import numpy as np, ml_dtypes
CORES = [10,34,74,98]
N = 4
import mx_ref
BF = ml_dtypes.bfloat16
def entries(a):
    return np.ascontiguousarray(a.T).reshape(-1)
def table(e):
    return np.ascontiguousarray(np.reshape(e, (-1, 16)).T).astype(np.int32)
def cols(t, e):
    v = np.concatenate([t.reshape(128, -1, 4), np.zeros((128, 1, 4), BF)], axis=1)
    return np.ascontiguousarray(v[:, e]).reshape(128, -1)
def cut(t, i, w=512):
    return t[:, w * i:w * i + w]
def f(rng, *shape):
    return mx_ref.flush((rng.standard_normal(shape, dtype=np.float32) * np.exp2(rng.integers(-2, 3, shape[:-1] + (1,)))).astype(BF))
def wide(rng, *shape, cols=0):
    v = rng.standard_normal(shape, dtype=np.float32) * np.exp2(rng.integers(-12, 13, shape)).astype(np.float32)
    if cols: v *= np.repeat(np.exp2(rng.integers(-cols, cols + 1, shape[:-2] + (1, shape[-1] // 4))) * (rng.random(shape[:-2] + (1, shape[-1] // 4)) > 0.0625), 4, axis=-1).astype(np.float32)
    return mx_ref.flush(v.astype(BF))
K, B, R, O, CO = 256, 32, 5, 2, 144
def others(d):
    return [s for s in range(N) if s != d]
def numbers_of(a):
    return np.stack([entries(e) for e in a]).reshape(N, R, N, B)
def batch(tab, cs, t, d):
    return np.concatenate([cols(tab[s], cs[s, t, d]) for s in others(d)], axis=1)
def passes(u, new):
    return int(np.sum(mx_ref.matmul(mx_ref.quantize(u), mx_ref.quantize(new))[0] >= 0))
def write(tab, new, keys):
    tab.reshape(128, K, 4)[:, keys] = new.reshape(128, -1, 4)
def level(rng, n, rule, must):
    if rule == "all": return min(n)
    if rule == "none": return max(n) + 1
    if rule == "edge": return max(n)
    v = min(n, key=lambda a: abs(2 * sum(b >= a for b in n) - N))
    low = max([a for a in n if a < v], default=v - 1)
    h = int(rng.integers(low + 1, v + 1))
    return min(h, n[must]) if rule == "chain" else h
def draw_key(rng, at, got, d):
    for _ in range(1000):
        k = int(rng.integers(0, K)); q = divmod(int(at[k]), K)[0]
        if q == d or got[at[k]] or got.reshape(N, K)[q].sum() < CO:
            got[at[k]] = True
            return k
    raise RuntimeError("no key")
def draw_new(rng, at, got, d, q):
    k = np.flatnonzero((at >= q * K) & (at < q * K + K) & ~got[at])
    if len(k) == 0 or got.reshape(N, K)[q].sum() >= CO: return draw_key(rng, at, got, d)
    k = int(rng.choice(k)); got[at[k]] = True
    return k
def game(rng, x, u, rule):
    cs, cd, thr = np.full((N, R, N, B), -1), np.full((N, R, N, B), -1), np.zeros(16, int)
    tab, at = np.array(x, order="C"), np.arange(N * K).reshape(N, K)
    got = np.zeros((N, N * K), bool)
    p, hold, done = rng.permutation(N), rng.permutation(K)[:B], 0
    one, told = int(rng.integers(0, R)), {"all": 0, "none": (N - 1) * B + 1, "chain": (N - 1) * B}
    if rule == "chain":
        got[:, p[0] * K + hold] = True
        u[int(p[(one + 1) % N])] = 0
    for t in range(R):
        a, e = int(p[t % N]), int(p[(t + 1) % N])
        for d in range(N):
            cd[d, t, others(d)] = rng.permutation(K)[:(N - 1) * B].reshape(N - 1, B)
            for s in others(d):
                if rule == "chain" and (s, d) == (a, e): cs[s, t, d] = hold
                elif rule == "all" and d == p[0]: cs[s, t, d] = [draw_new(rng, at[s], got[d], d, int(p[1])) for j in range(B)]
                else: cs[s, t, d] = [draw_key(rng, at[s], got[d], d) for j in range(B)]
        new = [batch(tab, cs, t, d) for d in range(N)]
        src = [np.concatenate([at[s, cs[s, t, d]] for s in others(d)]) for d in range(N)]
        n = [passes(u[d], new[d]) for d in range(N)]
        thr[t] = told[rule] if t == one and rule in told else level(rng, n, rule, e)
        for d in range(N):
            if n[d] >= thr[t]:
                keys = cd[d, t, others(d)].reshape(-1)
                write(tab[d], new[d], keys); at[d, keys] = src[d]; done += 1
        hold = cd[e, t, a]
    return cs, cd, thr, done, int(got[p[0]].reshape(N, K)[p[1]].sum())
def make(rng, rule="half", x=None):
    if x is None: x = f(rng, N, 128, 4 * K)
    u = np.zeros((N, 128, 512), BF); u[:, :, :4] = f(rng, N, 128, 4)
    w = f(rng, N, 128, 512 * R * O)
    for _ in range(50):
        cs, cd, thr, done, most = game(rng, x, u, rule)
        if (rule != "half" or N * R <= 3 * done <= 2 * N * R) and (rule != "all" or most == CO):
            return {"x": x, "u": u, "w": w, "cs": np.stack([table(e.reshape(-1)) for e in cs]), "cd": np.stack([table(e.reshape(-1)) for e in cd]), "thr": np.stack([table(thr) for r in range(N)])}
    raise RuntimeError("no draw")
def setup_inputs(rng):
    return make(rng)
def setup_inputs_all(rng):
    return make(rng, "all")
def setup_inputs_none(rng):
    return make(rng, "none")
def setup_inputs_edge(rng):
    return make(rng, "edge")
def setup_inputs_chain(rng):
    return make(rng, "chain")
def setup_inputs_spread(rng):
    x = np.array(wide(rng, N, 128, 4 * K, cols=6))
    x[np.abs(x.astype(np.float32)) < 2.0 ** -30] = 0
    return make(rng, "half", x)
def check_inputs(d):
    b = []
    for name in ("x", "u", "w"):
        v = np.abs(np.asarray(d[name]).astype(np.float32))
        if not (np.isfinite(v) & ((v == 0) | ((v >= 2.0 ** -30) & (v <= 2.0 ** 30)))).all(): b.append(name + ": a value that isn't finite, or neither zero nor 2**-30 to 2**30 in size")
    cs, cd = numbers_of(d["cs"]), numbers_of(d["cd"])
    for r in range(N):
        for t in range(R):
            if (cs[r, t, r] != -1).any() or (cd[r, t, r] != -1).any(): b.append("a rank's own part isn't -1")
            k, e = cs[r, t, others(r)], cd[r, t, others(r)].reshape(-1)
            if k.min() < 0 or k.max() >= K: b.append("cs")
            if e.min() < 0 or e.max() >= K or len(set(e.tolist())) != len(e): b.append("cd")
        h = entries(d["thr"][r])
        if (h != entries(d["thr"][0])).any(): b.append("thr isn't the same on every rank")
        if h.min() < 0 or h.max() > (N - 1) * B + 1 or (h[R:] != 0).any(): b.append("thr")
    if (np.asarray(d["u"])[:, :, 4:].astype(np.float32) != 0).any(): b.append("u")
    if b: return b
    tab, at = np.array(d["x"], order="C"), np.arange(N * K).reshape(N, K)
    got = np.zeros((N, N * K), bool)
    for t in range(R):
        new = [batch(tab, cs, t, r) for r in range(N)]
        src = [np.concatenate([at[s, cs[s, t, r]] for s in others(r)]) for r in range(N)]
        for r in range(N):
            if passes(d["u"][r], new[r]) >= entries(d["thr"][r])[t]:
                keys = cd[r, t, others(r)].reshape(-1)
                write(tab[r], new[r], keys); at[r, keys] = src[r]; got[r, src[r]] = True
    for r in range(N):
        for q in others(r):
            if got[r].reshape(N, K)[q].sum() > CO: b.append("too many columns of one rank are written on another")
    return b
def reference(x, u, w, cs, cd, thr):
    cs, cd = numbers_of(cs), numbers_of(cd)
    tab = np.array(x, order="C")
    y = np.zeros((N, 128, R * O * K), np.float32)
    for t in range(R):
        new = [batch(tab, cs, t, d) for d in range(N)]
        for d in range(N):
            if passes(u[d], new[d]) >= entries(thr[d])[t]: write(tab[d], new[d], cd[d, t, others(d)].reshape(-1))
            q = mx_ref.quantize(tab[d])
            for o in range(O):
                i = t * O + o
                y[d][:, K * i:K * i + K] = mx_ref.matmul(mx_ref.quantize(cut(w[d], i)), q)
    return {"y": y}

@@ -1,0 +1,318 @@
+from concourse.bass import DstId, RemoteDMATransfer
+from concourse.mybir import dt, AluOpType, ActivationFunctionType
+
+N, K, B, R, O = 4, 256, 32, 5, 2
+NB = (N - 1) * B
+LC = NB // 16
+KC = K // 16
+TW = 2 * K
+ZW = 32
+GW = 2 * NB
+LW = TW + ZW + GW
+NL = LW // 32
+
+SCRATCH = {
+    "xt": ("sbuf", [128, 4 * K], "bfloat16"),
+    "ut": ("sbuf", [128, 16], "bfloat16"),
+    "ur": ("sbuf", [128, 512], "bfloat16"),
+    "uqc": ("sbuf", [128, 128], "float8_e4m3fn_x4"),
+    "uqs": ("sbuf", [128, 128], "uint8"),
+    "wt": ("sbuf", [128, 512 * R * O], "bfloat16"),
+    "wqc": ("sbuf", [128, 128 * R * O], "float8_e4m3fn_x4"),
+    "wqs": ("sbuf", [128, 128 * R * O], "uint8"),
+    "csi": ("sbuf", [128, 8 * R], "int32"),
+    "cdi": ("sbuf", [128, 8 * R], "int32"),
+    "csc": ("sbuf", [128, LC * R], "int32"),
+    "cdc": ("sbuf", [128, LC * R], "int32"),
+    "csh": ("sbuf", [128, LC * R], "int32"),
+    "cdh": ("sbuf", [128, LC * R], "int32"),
+    "csp": ("sbuf", [128, LC * R], "float32"),
+    "cdp": ("sbuf", [128, LC * R], "float32"),
+    "cdo": ("sbuf", [128, LC * R], "uint16"),
+    "bo": ("sbuf", [128, 2 * LC * R], "uint16"),
+    "of0": ("sbuf", [128, LC], "uint16"),
+    "thr1": ("sbuf", [128, 16], "int32"),
+    "thb": ("sbuf", [128, 16], "int32"),
+    "hh": ("sbuf", [128, 16], "float32"),
+    "pidx": ("sbuf", [128, 32], "int32"),
+    "p3i": ("sbuf", [128, 32], "int32"),
+    "u3": ("sbuf", [128, 32], "uint16"),
+    "p15i": ("sbuf", [128, 1], "int32"),
+    "oddi": ("sbuf", [128, 1], "int32"),
+    "p15f": ("sbuf", [128, 1], "float32"),
+    "oddf": ("sbuf", [128, 1], "float32"),
+    "odd16": ("sbuf", [128, 1], "float32"),
+    "evf": ("sbuf", [128, 1], "float32"),
+    "zodd": ("sbuf", [128, 1], "float32"),
+    "zev": ("sbuf", [128, 1], "float32"),
+    "k16": ("sbuf", [128, KC], "float32"),
+    "keyb": ("sbuf", [128, KC], "float32"),
+    "jval": ("sbuf", [128, NB], "bfloat16"),
+    "lb": ("sbuf", [128, R * LW], "bfloat16"),
+    "tb": ("sbuf", [128, R * LW], "bfloat16"),
+    "lv": ("sbuf", [128, R * NL], "float32"),
+    "lm": ("sbuf", [128, R * NL], "float32"),
+    "ln": ("sbuf", [128, R * NL], "float32"),
+    "bs": ("sbuf", [128, R * NL], "float32"),
+    "nh": ("sbuf", [128, R * NL], "float32"),
+    "bh": ("sbuf", [128, R * NL], "float32"),
+    "mn": ("sbuf", [128, R * NL], "float32"),
+    "mx": ("sbuf", [128, R * NL], "float32"),
+    "off": ("sbuf", [128, R * 32], "uint16"),
+    "sg": ("sbuf", [128, R * NB], "float32"),
+    "cnt": ("sbuf", [128, R], "float32"),
+    "ysb": ("sbuf", [128, R * O * K], "float32"),
+    "psc": ("psum", [128, 1024], "float32"),
+    "psy": ("psum", [128, 3072], "float32"),
+}
+for _t in range(R):
+    SCRATCH["sndc%d" % _t] = ("sbuf", [128, NB], "float8_e4m3fn_x4")
+    SCRATCH["snds%d" % _t] = ("sbuf", [128, NB], "uint8")
+for _t in range(R + 1):
+    SCRATCH["winc%d" % _t] = ("sbuf", [128, K + NB], "float8_e4m3fn_x4")
+    SCRATCH["wins%d" % _t] = ("sbuf", [128, K + NB], "uint8")
+
+SEMAPHORES = ["xl", "csl", "cdl", "ul", "thl", "iot", "tbc", "u3r", "urr", "uq", "xq", "o0", "vq", "kq", "yl"]
+for _t in range(R):
+    SEMAPHORES += ["%s%d" % (n, _t) for n in ("arr", "snt", "pc", "ps", "tc", "ts", "sco", "act", "ofr", "wl", "wq", "ym", "ev", "ew")]
+
+AL = AluOpType
+AF = ActivationFunctionType
+
+
+def rank_program(g, core, T, topo):
+    r = T.rank_of(core)
+    if r is None:
+        return
+    others = [s for s in range(N) if s != r]
+    V, S, X, Y = g.vector, g.scalar, g.tensor, g.sync
+    total = {}
+    waited = {}
+
+    def up(call, name, n=1):
+        call.then_inc(T.sem[name], n)
+        total[name] = total.get(name, 0) + n
+
+    def wait(q, name):
+        q.wait_ge(T.sem[name], total[name])
+        waited[name] = total[name]
+
+    def v(call, name="vq"):
+        up(call, name)
+
+    def vw():
+        wait(V, "vq")
+
+    up(Y.dma_start(T.xt[:, :], T.x[:, :]), "xl", 16)
+    for a in range(4):
+        up(S.dma_start(T.csi[16 * a:16 * a + 16, :], T.cs[:, :]), "csl", 16)
+        up(Y.dma_start(T.csi[16 * a + 64:16 * a + 80, :], T.cs[:, :]), "csl", 16)
+    up(S.dma_start(T.ut[:, :], T.u[:, 0:16]), "ul", 16)
+    for a in range(4):
+        up(S.dma_start(T.cdi[16 * a:16 * a + 16, :], T.cd[:, :]), "cdl", 16)
+        up(Y.dma_start(T.cdi[16 * a + 64:16 * a + 80, :], T.cd[:, :]), "cdl", 16)
+    up(Y.dma_start(T.thr1[0:1, :], T.thr[:, :]), "thl", 16)
+
+    up(g.iota(T.pidx[:, :], [[0, 32]], 0, 1), "iot")
+    up(g.iota(T.k16[:, :], [[16, KC]], 0, 0, allow_small_or_imprecise_dtypes=True), "iot")
+    up(g.iota(T.jval[:, :], [[1, NB]], 1, 0, allow_small_or_imprecise_dtypes=True), "iot")
+    v(V.memset(T.lb[:, 0:LW], 0.0))
+    wait(V, "iot")
+    v(V.tensor_scalar(T.p3i[:, :], T.pidx[:, :], 3, None, AL.bitwise_and))
+    v(V.tensor_scalar(T.p15i[:, :], T.pidx[:, 0:1], 15, None, AL.bitwise_and))
+    v(V.tensor_scalar(T.oddi[:, :], T.pidx[:, 0:1], 4, 1, AL.logical_shift_right, AL.bitwise_and))
+    vw()
+    v(V.tensor_copy(T.u3[:, :], T.p3i[:, :]), "u3r")
+    v(V.tensor_copy(T.p15f[:, :], T.p15i[:, :]))
+    v(V.tensor_copy(T.oddf[:, :], T.oddi[:, :]))
+    vw()
+    v(V.tensor_scalar(T.keyb[:, :], T.k16[:, :], T.p15f[:, 0:1], None, AL.add))
+    v(V.tensor_scalar(T.odd16[:, :], T.oddf[:, :], 16.0, None, AL.mult))
+    v(V.tensor_scalar(T.evf[:, :], T.oddf[:, :], -1.0, 1.0, AL.mult, AL.add))
+    v(V.tensor_scalar(T.zodd[:, :], T.oddf[:, :], float(TW), None, AL.mult))
+    v(V.tensor_scalar(T.zev[:, :], T.oddf[:, :], float(16 - TW), float(TW), AL.mult, AL.add))
+
+    wait(V, "csl")
+    runs = []
+    if r > 0:
+        runs.append((0, 0, 2 * r))
+    if r < N - 1:
+        runs.append((2 * r + 2, 2 * r, LC - 2 * r))
+    for a, b, n in runs:
+        v(V.tensor_copy(T.of0[:, b:b + n], T.csi[:, a:a + n]), "o0")
+    wait(V, "xl")
+    v(V.quantize_mx(T.winc0[:, 0:K], T.wins0[:, 0:K], T.xt[:, :]), "xq")
+    wait(V, "o0")
+    wait(V, "xq")
+    v(V.tensor_copy(T.sndc0[:, :].bitcast(dt.uint32), T.winc0[:, 0:K].bitcast(dt.uint32).indirect(T.of0[:, :])), "pc0")
+    wait(S, "o0")
+    wait(S, "xq")
+    up(S.activation(T.snds0[:, :], T.wins0[:, 0:K].indirect(T.of0[:, :]), AF.Copy), "ps0")
+
+    def send(t):
+        for kind in ("c", "s"):
+            wait(g, "p%s%d" % (kind, t))
+            tr = []
+            for b, d in enumerate(others):
+                rid, pid, _ = topo.addr(d_core(d))
+                e = topo.engines(core, d_core(d))
+                i = 2 * ((b + (3 if kind == "s" else 0)) % (len(e) // 2))
+                at = K + B * (r if r < d else r - 1)
+                src = T["snd%s%d" % (kind, t)][:, B * b:B * b + B]
+                dst = T["win%s%d" % (kind, t)][:, at:at + B]
+                if kind == "c":
+                    src, dst = src.bitcast(dt.uint8), dst.bitcast(dt.uint8)
+                tr.append(RemoteDMATransfer(dst_ids=[DstId(rid=rid, pnc=pid)], dma_engine_mask=(1 << e[i]) + (1 << e[i + 1]),
+                                            remote_sem=T.sem["arr%d" % t], srcs=[src], dsts=[dst]))
+            g.remote_dma_fused(tr, local_sem=T.sem["snt%d" % t])
+        total["snt%d" % t] = 2 * 2 * len(others)
+        total["arr%d" % t] = 2 * 2 * len(others)
+
+    def d_core(d):
+        return T.cores[d]
+
+    send(0)
+
+    wait(S, "u3r")
+    wait(S, "ul")
+    up(S.activation(T.ur[:, :], T.ut[:, :].indirect(T.u3[:, :]), AF.Copy), "urr")
+    wait(V, "urr")
+    v(V.quantize_mx(T.uqc[:, :], T.uqs[:, :], T.ur[:, :]), "uq")
+
+    wait(g, "thl")
+    up(g.partition_broadcast(T.thb[:, :], T.thr1[0:1, :], 128), "tbc")
+
+    wait(V, "cdl")
+    for src, dst in (("cdi", "cdc"), ("csi", "csc")):
+        for a, b, n in runs:
+            for i in range(n):
+                v(V.tensor_copy(T[dst][:, b + i:LC * R:LC], T[src][:, a + i:8 * R:8]))
+    vw()
+    v(V.tensor_scalar(T.cdh[:, :], T.cdc[:, :], 240, None, AL.bitwise_and))
+    v(V.tensor_scalar(T.csh[:, :], T.csc[:, :], 240, None, AL.bitwise_and))
+    vw()
+    v(V.tensor_tensor(T.cdp[:, :], T.cdc[:, :], T.cdh[:, :], AL.add))
+    v(V.tensor_tensor(T.csp[:, :], T.csc[:, :], T.csh[:, :], AL.add))
+    vw()
+    v(V.tensor_scalar(T.cdo[:, :], T.cdp[:, :], T.odd16[:, 0:1], None, AL.add))
+    v(V.tensor_scalar(T.bo[:, 0:2 * LC * R:2], T.csp[:, :], T.evf[:, 0:1], T.zodd[:, 0:1], AL.mult, AL.add))
+    v(V.tensor_scalar(T.bo[:, 1:2 * LC * R:2], T.csp[:, :], T.oddf[:, 0:1], T.zev[:, 0:1], AL.mult, AL.add))
+    wait(V, "tbc")
+    v(V.tensor_scalar(T.hh[:, :], T.thb[:, :], 2.0, float(-NB - 1), AL.mult, AL.add))
+    for t in range(R):
+        z = NL * t
+        v(V.tensor_copy(T.bs[:, z:z + KC], T.keyb[:, :]))
+        if t + 1 < R:
+            v(V.tensor_copy(T.bs[:, z + KC + 1:z + NL], T.csc[:, LC * (t + 1):LC * (t + 2)]))
+
+    def lists(t):
+        z, q = LW * t, NL * t
+        w = LW if t + 1 < R else TW
+        n = NL if t + 1 < R else KC
+        vw()
+        v(V.tensor_copy(T.lb[:, z:z + TW].indirect(T.cdo[:, LC * t:LC * t + LC]), T.jval[:, :]))
+        if t + 1 < R:
+            vw()
+            v(V.tensor_copy(T.lb[:, z + TW + ZW:z + LW], T.lb[:, z:z + TW + ZW].indirect(T.bo[:, 2 * LC * (t + 1):2 * LC * (t + 2)])))
+        vw()
+        v(V.transpose(T.tb[:, z:z + w], T.lb[:, z:z + w]))
+        vw()
+        v(V.tensor_tensor(T.lv[:, q:q + n], T.tb[:, z:z + w:32], T.tb[:, z + 16:z + w:32], AL.add))
+        if t + 1 < R:
+            v(V.memset(T.bs[:, q + KC:q + KC + 1], 0.0))
+        vw()
+        v(V.tensor_scalar(T.lm[:, q:q + n], T.lv[:, q:q + n], 1.0, float(K - 1), AL.min, AL.mult))
+        v(V.tensor_scalar(T.bh[:, q:q + n], T.bs[:, q:q + n], 1.0 / 512, T.hh[:, t:t + 1], AL.mult, AL.add))
+        vw()
+        v(V.tensor_tensor(T.ln[:, q:q + n], T.lv[:, q:q + n], T.lm[:, q:q + n], AL.add))
+        vw()
+        v(V.tensor_scalar(T.nh[:, q:q + n], T.ln[:, q:q + n], 1.0 / 512, T.hh[:, t:t + 1], AL.mult, AL.add))
+
+    lists(0)
+    v(V.memset(T.lb[:, LW:R * LW], 0.0))
+
+    def load_w(t):
+        up(Y.dma_start(T.wt[:, 1024 * t:1024 * t + 1024], T.w[:, 1024 * t:1024 * t + 1024]), "wl%d" % t, 16)
+
+    def quantize_w(t):
+        wait(V, "wl%d" % t)
+        for i in (2 * t, 2 * t + 1):
+            v(V.quantize_mx(T.wqc[:, 128 * i:128 * i + 128], T.wqs[:, 128 * i:128 * i + 128], T.wt[:, 512 * i:512 * i + 512]), "wq%d" % t)
+
+    wait(Y, "snt0")
+    for t in (0, 1, 2):
+        load_w(t)
+
+    for t in range(R):
+        last = t + 1 == R
+        q, z = NL * t, 32 * t
+        n = KC if last else NL
+        wc, ws = T["winc%d" % t], T["wins%d" % t]
+        wait(X, "uq")
+        if t == 0:
+            wait(X, "xq")
+        wait(X, "arr%d" % t)
+        a = K + NB - 128
+        bank = 512 * (t % 2)
+        up(X.matmul_mx(T.psc[:, bank:bank + 128], T.uqc[:, :], T.uqs[:, :], wc[:, a:K + NB], ws[:, a:K + NB], True, True), "sco%d" % t)
+        wait(S, "sco%d" % t)
+        up(S.activation(T.sg[:, NB * t:NB * t + NB], T.psc[:, bank + 128 - NB:bank + 128], AF.Sign, bias=1e-30, accum_out=T.cnt[:, t:t + 1]), "act%d" % t)
+        vw()
+        wait(V, "act%d" % t)
+        v(V.tensor_scalar(T.mn[:, q:q + n], T.nh[:, q:q + n], T.cnt[:, t:t + 1], None, AL.min))
+        vw()
+        v(V.tensor_tensor(T.mx[:, q:q + n], T.mn[:, q:q + n], T.bh[:, q:q + n], AL.max))
+        vw()
+        if not last:
+            v(V.tensor_scalar(T.off[:, z + KC + 1:z + KC + 2 + LC - 1], T.mx[:, q + KC + 1:q + NL], T.hh[:, t:t + 1], 512.0, AL.subtract, AL.mult), "ofr%d" % t) if False else None
+            v(V.tensor_scalar(T.off[:, z + KC:z + KC + LC], T.mx[:, q + KC + 1:q + NL], T.hh[:, t:t + 1], 512.0, AL.subtract, AL.mult), "ofr%d" % t)
+            wait(V, "ofr%d" % t)
+            oc = T.off[:, z + KC:z + KC + LC]
+            v(V.tensor_copy(T["sndc%d" % (t + 1)][:, :].bitcast(dt.uint32), wc[:, 0:K + NB].bitcast(dt.uint32).indirect(oc)), "pc%d" % (t + 1))
+            wait(S, "ofr%d" % t)
+            up(S.activation(T["snds%d" % (t + 1)][:, :], ws[:, 0:K + NB].indirect(oc), AF.Copy), "ps%d" % (t + 1))
+            send(t + 1)
+        v(V.tensor_scalar(T.off[:, z:z + KC], T.mx[:, q:q + KC], T.hh[:, t:t + 1], 512.0, AL.subtract, AL.mult), "ew%d" % t)
+        wait(V, "ew%d" % t)
+        wait(S, "ew%d" % t)
+        oc = T.off[:, z:z + KC]
+        nc, ns = T["winc%d" % (t + 1)], T["wins%d" % (t + 1)]
+        v(V.tensor_copy(nc[:, 0:K].bitcast(dt.uint32), wc[:, 0:K + NB].bitcast(dt.uint32).indirect(oc)), "tc%d" % t)
+        up(S.activation(ns[:, 0:K], ws[:, 0:K + NB].indirect(oc), AF.Copy), "ts%d" % t)
+        if not last:
+            lists(t + 1)
+        for k in ((0,), (1, 2), (3,), (4,), ())[t]:
+            quantize_w(k)
+        wait(X, "tc%d" % t)
+        wait(X, "ts%d" % t)
+        wait(X, "wq%d" % t)
+        if t >= 3:
+            wait(X, "ev%d" % (t - 3))
+        for o in range(O):
+            i = O * t + o
+            p = 512 * (i % 6)
+            up(X.matmul_mx(T.psy[:, p:p + K], T.wqc[:, 128 * i:128 * i + 128], T.wqs[:, 128 * i:128 * i + 128], nc[:, 0:K], ns[:, 0:K], True, True), "ym%d" % t)
+        wait(S, "ym%d" % t)
+        for o in range(O):
+            i = O * t + o
+            p = 512 * (i % 6)
+            if last and o == 1:
+                wait(V, "ym%d" % t)
+                v(V.tensor_copy(T.ysb[:, K * i:K * i + K], T.psy[:, p:p + K]))
+            else:
+                up(S.activation(T.ysb[:, K * i:K * i + K], T.psy[:, p:p + K], AF.Copy), "ev%d" % t)
+        if not last:
+            wait(Y, "snt%d" % (t + 1))
+            if t == 0:
+                load_w(3)
+                load_w(4)
+            wait(Y, "ev%d" % t)
+            up(Y.dma_start(T.y[:, O * K * t:O * K * (t + 1)], T.ysb[:, O * K * t:O * K * (t + 1)]), "yl", 16)
+        else:
+            wait(Y, "vq")
+            up(Y.dma_start(T.y[:, K * (2 * t + 1):K * (2 * t + 2)], T.ysb[:, K * (2 * t + 1):K * (2 * t + 2)]), "yl", 16)
+            wait(S, "ev%d" % t)
+            up(S.dma_start(T.y[:, K * 2 * t:K * (2 * t + 1)], T.ysb[:, K * 2 * t:K * (2 * t + 1)]), "kq", 16)
+    for name in total:
+        if waited.get(name, 0) < total[name]:
+            wait(Y, name)

@@ -5,76 +5,43 @@ N, K, B, R, O = 4, 256, 32, 5, 2
 NB = (N - 1) * B
 LC = NB // 16
 KC = K // 16
-TW = 2 * K
 ZW = 32
+TW = 2 * K
 GW = 2 * NB
-LW = TW + ZW + GW
-NL = LW // 32
+LW = ZW + TW + GW
+NL = KC + LC
+HK = K // 2
+WIN = NB + K
+RL = R * LC
 
 SCRATCH = {
-    "xt": ("sbuf", [128, 4 * K], "bfloat16"),
-    "ut": ("sbuf", [128, 16], "bfloat16"),
-    "ur": ("sbuf", [128, 512], "bfloat16"),
-    "uqc": ("sbuf", [128, 128], "float8_e4m3fn_x4"),
-    "uqs": ("sbuf", [128, 128], "uint8"),
-    "wt": ("sbuf", [128, 512 * R * O], "bfloat16"),
-    "wqc": ("sbuf", [128, 128 * R * O], "float8_e4m3fn_x4"),
-    "wqs": ("sbuf", [128, 128 * R * O], "uint8"),
-    "csi": ("sbuf", [128, 8 * R], "int32"),
-    "cdi": ("sbuf", [128, 8 * R], "int32"),
-    "csc": ("sbuf", [128, LC * R], "int32"),
-    "cdc": ("sbuf", [128, LC * R], "int32"),
-    "csh": ("sbuf", [128, LC * R], "int32"),
-    "cdh": ("sbuf", [128, LC * R], "int32"),
-    "csp": ("sbuf", [128, LC * R], "float32"),
-    "cdp": ("sbuf", [128, LC * R], "float32"),
-    "cdo": ("sbuf", [128, LC * R], "uint16"),
-    "bo": ("sbuf", [128, 2 * LC * R], "uint16"),
-    "of0": ("sbuf", [128, LC], "uint16"),
-    "thr1": ("sbuf", [128, 16], "int32"),
-    "thb": ("sbuf", [128, 16], "int32"),
-    "hh": ("sbuf", [128, 16], "float32"),
-    "pidx": ("sbuf", [128, 32], "int32"),
-    "p3i": ("sbuf", [128, 32], "int32"),
-    "u3": ("sbuf", [128, 32], "uint16"),
-    "p15i": ("sbuf", [128, 1], "int32"),
-    "oddi": ("sbuf", [128, 1], "int32"),
-    "p15f": ("sbuf", [128, 1], "float32"),
-    "oddf": ("sbuf", [128, 1], "float32"),
-    "odd16": ("sbuf", [128, 1], "float32"),
-    "evf": ("sbuf", [128, 1], "float32"),
-    "zodd": ("sbuf", [128, 1], "float32"),
-    "zev": ("sbuf", [128, 1], "float32"),
-    "k16": ("sbuf", [128, KC], "float32"),
-    "keyb": ("sbuf", [128, KC], "float32"),
-    "jval": ("sbuf", [128, NB], "bfloat16"),
-    "lb": ("sbuf", [128, R * LW], "bfloat16"),
-    "tb": ("sbuf", [128, R * LW], "bfloat16"),
-    "lv": ("sbuf", [128, R * NL], "float32"),
-    "lm": ("sbuf", [128, R * NL], "float32"),
-    "ln": ("sbuf", [128, R * NL], "float32"),
-    "bs": ("sbuf", [128, R * NL], "float32"),
-    "nh": ("sbuf", [128, R * NL], "float32"),
-    "bh": ("sbuf", [128, R * NL], "float32"),
-    "mn": ("sbuf", [128, R * NL], "float32"),
-    "mx": ("sbuf", [128, R * NL], "float32"),
-    "off": ("sbuf", [128, R * 32], "uint16"),
-    "sg": ("sbuf", [128, R * NB], "float32"),
-    "cnt": ("sbuf", [128, R], "float32"),
-    "ysb": ("sbuf", [128, R * O * K], "float32"),
     "psc": ("psum", [128, 1024], "float32"),
     "psy": ("psum", [128, 3072], "float32"),
 }
+for _n, _w, _d in (
+        ("xt", 4 * K, "bfloat16"), ("ut", 16, "bfloat16"), ("ur", 512, "bfloat16"), ("uqc", 128, "float8_e4m3fn_x4"), ("uqs", 128, "uint8"),
+        ("wt", 512 * R * O, "bfloat16"), ("wqc", 128 * R * O, "float8_e4m3fn_x4"), ("wqs", 128 * R * O, "uint8"),
+        ("csi", 8 * R, "int32"), ("cdi", 8 * R, "int32"), ("csc", RL, "int32"), ("cdc", RL, "int32"), ("csh", RL, "int32"), ("cdh", RL, "int32"),
+        ("csp", RL, "float32"), ("cdp", RL, "float32"), ("bun", 4 * RL, "uint16"), ("of0", LC, "uint16"),
+        ("thr1", 16, "int32"), ("thb", 16, "int32"), ("hh", 16, "float32"), ("hn", 16, "float32"), ("hb", 16, "float32"),
+        ("pidx", 32, "int32"), ("p3i", 32, "int32"), ("u3", 32, "uint16"),
+        ("p15i", 1, "int32"), ("oddi", 1, "int32"), ("p15f", 1, "float32"), ("oddf", 1, "float32"), ("odd16", 1, "float32"), ("evf", 1, "float32"),
+        ("zodd", 1, "float32"), ("zev", 1, "float32"), ("k16", KC, "float32"), ("keyb", KC, "float32"), ("jval", NB, "bfloat16"),
+        ("lb", R * LW, "bfloat16"), ("tb", R * 32 * NL, "bfloat16"), ("lv", R * NL, "float32"),
+        ("nh", R * NL, "float32"), ("bh", R * NL, "float32"), ("mn", R * NL, "float32"), ("mx", R * NL, "float32"),
+        ("off", R * 32, "uint16"), ("sg", R * NB, "float32"), ("cnt", R, "float32"), ("ysb", R * O * K, "float32")):
+    SCRATCH[_n] = ("sbuf", [128, _w], _d)
 for _t in range(R):
     SCRATCH["sndc%d" % _t] = ("sbuf", [128, NB], "float8_e4m3fn_x4")
     SCRATCH["snds%d" % _t] = ("sbuf", [128, NB], "uint8")
 for _t in range(R + 1):
-    SCRATCH["winc%d" % _t] = ("sbuf", [128, K + NB], "float8_e4m3fn_x4")
-    SCRATCH["wins%d" % _t] = ("sbuf", [128, K + NB], "uint8")
+    SCRATCH["winc%d" % _t] = ("sbuf", [128, WIN], "float8_e4m3fn_x4")
+    SCRATCH["wins%d" % _t] = ("sbuf", [128, WIN], "uint8")
 
 SEMAPHORES = ["xl", "csl", "cdl", "ul", "thl", "iot", "tbc", "u3r", "urr", "uq", "xq", "o0", "vq", "kq", "yl"]
 for _t in range(R):
-    SEMAPHORES += ["%s%d" % (n, _t) for n in ("arr", "snt", "pc", "ps", "tc", "ts", "sco", "act", "ofr", "wl", "wq", "ym", "ev", "ew")]
+    SEMAPHORES += ["%s%d" % (n, _t) for n in ("arr", "snt", "pc", "ps", "tc", "ts", "sco", "act", "ofr", "wl", "wq", "ym", "ev", "ew", "sc", "gt")]
+SEMAPHORES += ["%s%d%d" % (n, h, o) for n in ("lm", "le") for h in range(2) for o in range(O)] + ["lc0", "lc1", "ls0", "ls1"]
 
 AL = AluOpType
 AF = ActivationFunctionType
@@ -104,19 +71,21 @@ def rank_program(g, core, T, topo):
         wait(V, "vq")
 
     up(Y.dma_start(T.xt[:, :], T.x[:, :]), "xl", 16)
-    for a in range(4):
-        up(S.dma_start(T.csi[16 * a:16 * a + 16, :], T.cs[:, :]), "csl", 16)
-        up(Y.dma_start(T.csi[16 * a + 64:16 * a + 80, :], T.cs[:, :]), "csl", 16)
-    up(S.dma_start(T.ut[:, :], T.u[:, 0:16]), "ul", 16)
-    for a in range(4):
-        up(S.dma_start(T.cdi[16 * a:16 * a + 16, :], T.cd[:, :]), "cdl", 16)
-        up(Y.dma_start(T.cdi[16 * a + 64:16 * a + 80, :], T.cd[:, :]), "cdl", 16)
-    up(Y.dma_start(T.thr1[0:1, :], T.thr[:, :]), "thl", 16)
+    up(S.dma_start(T.csi[0:16, :], T.cs[:, :]), "csl", 16)
+    up(S.dma_start(T.csi[16:32, :], T.cs[:, :]), "csl", 16)
+    up(S.dma_start(T.thr1[0:1, :], T.thr[:, :]), "thl", 16)
+    up(Y.dma_start(T.ut[:, :], T.u[:, 0:16]), "ul", 16)
+    up(Y.dma_start(T.cdi[0:16, :], T.cd[:, :]), "cdl", 16)
+    up(Y.dma_start(T.cdi[16:32, :], T.cd[:, :]), "cdl", 16)
 
     up(g.iota(T.pidx[:, :], [[0, 32]], 0, 1), "iot")
     up(g.iota(T.k16[:, :], [[16, KC]], 0, 0, allow_small_or_imprecise_dtypes=True), "iot")
-    up(g.iota(T.jval[:, :], [[1, NB]], 1, 0, allow_small_or_imprecise_dtypes=True), "iot")
-    v(V.memset(T.lb[:, 0:LW], 0.0))
+    up(g.iota(T.jval[:, :], [[1, NB]], 0, 0, allow_small_or_imprecise_dtypes=True), "iot")
+
+    def fill(t):
+        v(V.memset(T.lb[:, LW * t:LW * t + ZW + TW], 512.0))
+
+    fill(0)
     wait(V, "iot")
     v(V.tensor_scalar(T.p3i[:, :], T.pidx[:, :], 3, None, AL.bitwise_and))
     v(V.tensor_scalar(T.p15i[:, :], T.pidx[:, 0:1], 15, None, AL.bitwise_and))
@@ -129,107 +98,117 @@ def rank_program(g, core, T, topo):
     v(V.tensor_scalar(T.keyb[:, :], T.k16[:, :], T.p15f[:, 0:1], None, AL.add))
     v(V.tensor_scalar(T.odd16[:, :], T.oddf[:, :], 16.0, None, AL.mult))
     v(V.tensor_scalar(T.evf[:, :], T.oddf[:, :], -1.0, 1.0, AL.mult, AL.add))
-    v(V.tensor_scalar(T.zodd[:, :], T.oddf[:, :], float(TW), None, AL.mult))
-    v(V.tensor_scalar(T.zev[:, :], T.oddf[:, :], float(16 - TW), float(TW), AL.mult, AL.add))
+    v(V.tensor_scalar(T.zodd[:, :], T.oddf[:, :], float(16 + ZW), None, AL.mult))
+    v(V.tensor_scalar(T.zev[:, :], T.oddf[:, :], float(-ZW), float(ZW), AL.mult, AL.add))
+    for t in range(1, R):
+        fill(t)
 
-    wait(V, "csl")
+    wait(g, "thl")
+    up(g.partition_broadcast(T.thb[:, :], T.thr1[0:1, :], 128), "tbc")
+
     runs = []
     if r > 0:
         runs.append((0, 0, 2 * r))
     if r < N - 1:
         runs.append((2 * r + 2, 2 * r, LC - 2 * r))
-    for a, b, n in runs:
-        v(V.tensor_copy(T.of0[:, b:b + n], T.csi[:, a:a + n]), "o0")
+
+    def compact(dst, src):
+        for a, b, n in runs:
+            for i in range(n):
+                v(V.tensor_copy(T[dst][0:32, b + i:RL:LC], T[src][0:32, a + i:8 * R:8]))
+
+    wait(V, "csl")
+    for k in range(0, 128, 32):
+        for a, b, n in runs:
+            v(V.tensor_copy(T.of0[k:k + 32, b:b + n], T.csi[0:32, a:a + n]), "o0")
+    compact("csc", "csi")
     wait(V, "xl")
-    v(V.quantize_mx(T.winc0[:, 0:K], T.wins0[:, 0:K], T.xt[:, :]), "xq")
+    v(V.quantize_mx(T.winc0[:, NB:WIN], T.wins0[:, NB:WIN], T.xt[:, :]), "xq")
     wait(V, "o0")
     wait(V, "xq")
-    v(V.tensor_copy(T.sndc0[:, :].bitcast(dt.uint32), T.winc0[:, 0:K].bitcast(dt.uint32).indirect(T.of0[:, :])), "pc0")
+    v(V.tensor_copy(T.sndc0[:, :].bitcast(dt.uint32), T.winc0[:, NB:WIN].bitcast(dt.uint32).indirect(T.of0[:, :])), "pc0")
     wait(S, "o0")
     wait(S, "xq")
-    up(S.activation(T.snds0[:, :], T.wins0[:, 0:K].indirect(T.of0[:, :]), AF.Copy), "ps0")
+    up(S.activation(T.snds0[:, :], T.wins0[:, NB:WIN].indirect(T.of0[:, :]), AF.Copy), "ps0")
+
+    def piece(kind, t, b, first, n):
+        d = others[b]
+        to = T.cores[d]
+        rid, pid, _ = topo.addr(to)
+        at = B * (r if r < d else r - 1)
+        src = T["snd%s%d" % (kind, t)][:, B * b:B * b + B]
+        dst = T["win%s%d" % (kind, t)][:, at:at + B]
+        if kind == "c":
+            src, dst = src.bitcast(dt.uint8), dst.bitcast(dt.uint8)
+        return RemoteDMATransfer(dst_ids=[DstId(rid=rid, pnc=pid)], dma_engine_mask=sum(1 << e for e in topo.engines(core, to)[first:first + n]),
+                                 remote_sem=T.sem["arr%d" % t], srcs=[src], dsts=[dst])
+
+    PLAN = (("c", ((0, 0, 2), (1, 2, 2), (2, 4, 2))), ("s", ((0, 6, 2),)), ("s", ((1, 0, 4), (2, 4, 4))))
 
     def send(t):
-        for kind in ("c", "s"):
+        n = 0
+        for kind, tr in PLAN:
             wait(g, "p%s%d" % (kind, t))
-            tr = []
-            for b, d in enumerate(others):
-                rid, pid, _ = topo.addr(d_core(d))
-                e = topo.engines(core, d_core(d))
-                i = 2 * ((b + (3 if kind == "s" else 0)) % (len(e) // 2))
-                at = K + B * (r if r < d else r - 1)
-                src = T["snd%s%d" % (kind, t)][:, B * b:B * b + B]
-                dst = T["win%s%d" % (kind, t)][:, at:at + B]
-                if kind == "c":
-                    src, dst = src.bitcast(dt.uint8), dst.bitcast(dt.uint8)
-                tr.append(RemoteDMATransfer(dst_ids=[DstId(rid=rid, pnc=pid)], dma_engine_mask=(1 << e[i]) + (1 << e[i + 1]),
-                                            remote_sem=T.sem["arr%d" % t], srcs=[src], dsts=[dst]))
-            g.remote_dma_fused(tr, local_sem=T.sem["snt%d" % t])
-        total["snt%d" % t] = 2 * 2 * len(others)
-        total["arr%d" % t] = 2 * 2 * len(others)
-
-    def d_core(d):
-        return T.cores[d]
+            g.remote_dma_fused([piece(kind, t, *p) for p in tr], local_sem=T.sem["snt%d" % t])
+            n += sum(p[2] for p in tr)
+        total["snt%d" % t] = n
+        total["arr%d" % t] = sum(p[2] for s in others for _, tr in PLAN for p in tr if [d for d in range(N) if d != s][p[0]] == r)
 
     send(0)
 
     wait(S, "u3r")
     wait(S, "ul")
     up(S.activation(T.ur[:, :], T.ut[:, :].indirect(T.u3[:, :]), AF.Copy), "urr")
-    wait(V, "urr")
-    v(V.quantize_mx(T.uqc[:, :], T.uqs[:, :], T.ur[:, :]), "uq")
 
-    wait(g, "thl")
-    up(g.partition_broadcast(T.thb[:, :], T.thr1[0:1, :], 128), "tbc")
-
+    q0 = slice(0, 32)
     wait(V, "cdl")
-    for src, dst in (("cdi", "cdc"), ("csi", "csc")):
-        for a, b, n in runs:
-            for i in range(n):
-                v(V.tensor_copy(T[dst][:, b + i:LC * R:LC], T[src][:, a + i:8 * R:8]))
+    compact("cdc", "cdi")
     vw()
-    v(V.tensor_scalar(T.cdh[:, :], T.cdc[:, :], 240, None, AL.bitwise_and))
-    v(V.tensor_scalar(T.csh[:, :], T.csc[:, :], 240, None, AL.bitwise_and))
+    v(V.tensor_scalar(T.cdh[q0, :], T.cdc[q0, :], 240, None, AL.bitwise_and))
+    v(V.tensor_scalar(T.csh[q0, :], T.csc[q0, :], 240, None, AL.bitwise_and))
+    v(V.tensor_copy(T.bun[q0, 3 * RL:4 * RL], T.csc[q0, :]))
     vw()
-    v(V.tensor_tensor(T.cdp[:, :], T.cdc[:, :], T.cdh[:, :], AL.add))
-    v(V.tensor_tensor(T.csp[:, :], T.csc[:, :], T.csh[:, :], AL.add))
+    v(V.tensor_tensor(T.cdp[q0, :], T.cdc[q0, :], T.cdh[q0, :], AL.add))
+    v(V.tensor_tensor(T.csp[q0, :], T.csc[q0, :], T.csh[q0, :], AL.add))
     vw()
-    v(V.tensor_scalar(T.cdo[:, :], T.cdp[:, :], T.odd16[:, 0:1], None, AL.add))
-    v(V.tensor_scalar(T.bo[:, 0:2 * LC * R:2], T.csp[:, :], T.evf[:, 0:1], T.zodd[:, 0:1], AL.mult, AL.add))
-    v(V.tensor_scalar(T.bo[:, 1:2 * LC * R:2], T.csp[:, :], T.oddf[:, 0:1], T.zev[:, 0:1], AL.mult, AL.add))
+    v(V.tensor_scalar(T.bun[q0, 0:RL], T.cdp[q0, :], T.odd16[q0, 0:1], None, AL.add))
+    v(V.tensor_scalar(T.bun[q0, RL:3 * RL:2], T.csp[q0, :], T.evf[q0, 0:1], T.zev[q0, 0:1], AL.mult, AL.add))
+    v(V.tensor_scalar(T.bun[q0, RL + 1:3 * RL:2], T.csp[q0, :], T.oddf[q0, 0:1], T.zodd[q0, 0:1], AL.mult, AL.add))
+    vw()
+    for k in (32, 64, 96):
+        v(V.tensor_copy(T.bun[k:k + 32, :], T.bun[q0, :]))
     wait(V, "tbc")
     v(V.tensor_scalar(T.hh[:, :], T.thb[:, :], 2.0, float(-NB - 1), AL.mult, AL.add))
-    for t in range(R):
-        z = NL * t
-        v(V.tensor_copy(T.bs[:, z:z + KC], T.keyb[:, :]))
-        if t + 1 < R:
-            v(V.tensor_copy(T.bs[:, z + KC + 1:z + NL], T.csc[:, LC * (t + 1):LC * (t + 2)]))
+    v(V.tensor_scalar(T.hn[:, :], T.thb[:, :], -2.0, float(NB), AL.mult, AL.add))
+    v(V.tensor_scalar(T.hb[:, :], T.thb[:, :], -2.0, NB + 1 + NB / 512.0, AL.mult, AL.add))
 
-    def lists(t):
+    def lists_begin(t):
         z, q = LW * t, NL * t
-        w = LW if t + 1 < R else TW
-        n = NL if t + 1 < R else KC
         vw()
-        v(V.tensor_copy(T.lb[:, z:z + TW].indirect(T.cdo[:, LC * t:LC * t + LC]), T.jval[:, :]))
+        v(V.tensor_copy(T.lb[:, z + ZW:z + ZW + TW].indirect(T.bun[:, LC * t:LC * t + LC]), T.jval[:, :]), "sc%d" % t)
+        h = T.hb[:, t:t + 1]
+        v(V.tensor_scalar(T.bh[:, q:q + KC], T.keyb[:, :], 1.0 / 512, h, AL.mult, AL.add))
         if t + 1 < R:
-            vw()
-            v(V.tensor_copy(T.lb[:, z + TW + ZW:z + LW], T.lb[:, z:z + TW + ZW].indirect(T.bo[:, 2 * LC * (t + 1):2 * LC * (t + 2)])))
-        vw()
-        v(V.transpose(T.tb[:, z:z + w], T.lb[:, z:z + w]))
-        vw()
-        v(V.tensor_tensor(T.lv[:, q:q + n], T.tb[:, z:z + w:32], T.tb[:, z + 16:z + w:32], AL.add))
-        if t + 1 < R:
-            v(V.memset(T.bs[:, q + KC:q + KC + 1], 0.0))
-        vw()
-        v(V.tensor_scalar(T.lm[:, q:q + n], T.lv[:, q:q + n], 1.0, float(K - 1), AL.min, AL.mult))
-        v(V.tensor_scalar(T.bh[:, q:q + n], T.bs[:, q:q + n], 1.0 / 512, T.hh[:, t:t + 1], AL.mult, AL.add))
-        vw()
-        v(V.tensor_tensor(T.ln[:, q:q + n], T.lv[:, q:q + n], T.lm[:, q:q + n], AL.add))
-        vw()
-        v(V.tensor_scalar(T.nh[:, q:q + n], T.ln[:, q:q + n], 1.0 / 512, T.hh[:, t:t + 1], AL.mult, AL.add))
+            v(V.tensor_scalar(T.bh[:, q + KC:q + NL], T.bun[:, 3 * RL + LC * (t + 1):3 * RL + LC * (t + 2)], 1.0 / 512, h, AL.mult, AL.add))
+            wait(S, "sc%d" % t)
+            up(S.activation(T.lb[:, z + ZW + TW:z + LW], T.lb[:, z:z + ZW + TW].indirect(T.bun[:, RL + 2 * LC * (t + 1):RL + 2 * LC * (t + 2)]), AF.Copy), "gt%d" % t)
 
-    lists(0)
-    v(V.memset(T.lb[:, LW:R * LW], 0.0))
+    def lists_end(t):
+        z, q, y = LW * t, NL * t, 32 * NL * t
+        n = NL if t + 1 < R else KC
+        wait(V, "sc%d" % t)
+        if t + 1 < R:
+            wait(V, "gt%d" % t)
+        v(V.transpose(T.tb[:, y:y + 32 * n], T.lb[:, z + ZW:z + ZW + 32 * n]))
+        vw()
+        v(V.tensor_tensor(T.lv[:, q:q + n], T.tb[:, y:y + 32 * n:32], T.tb[:, y + 16:y + 32 * n:32], AL.add))
+        vw()
+        v(V.tensor_scalar(T.nh[:, q:q + n], T.lv[:, q:q + n], 1.0 / 512, T.hn[:, t:t + 1], AL.mult, AL.add))
+
+    lists_begin(0)
+    wait(V, "urr")
+    v(V.quantize_mx(T.uqc[:, :], T.uqs[:, :], T.ur[:, :]), "uq")
+    lists_end(0)
 
     def load_w(t):
         up(Y.dma_start(T.wt[:, 1024 * t:1024 * t + 1024], T.w[:, 1024 * t:1024 * t + 1024]), "wl%d" % t, 16)
@@ -239,50 +218,56 @@ def rank_program(g, core, T, topo):
         for i in (2 * t, 2 * t + 1):
             v(V.quantize_mx(T.wqc[:, 128 * i:128 * i + 128], T.wqs[:, 128 * i:128 * i + 128], T.wt[:, 512 * i:512 * i + 512]), "wq%d" % t)
 
+    def product(i, bank, cols, win, name):
+        p = 512 * bank
+        a, b = NB + cols[0], NB + cols[1]
+        up(X.matmul_mx(T.psy[:, p:p + b - a], T.wqc[:, 128 * i:128 * i + 128], T.wqs[:, 128 * i:128 * i + 128], win[0][:, a:b], win[1][:, a:b], True, True), name)
+
     wait(Y, "snt0")
-    for t in (0, 1, 2):
-        load_w(t)
+    load_w(0)
+    load_w(1)
 
     for t in range(R):
         last = t + 1 == R
         q, z = NL * t, 32 * t
         n = KC if last else NL
         wc, ws = T["winc%d" % t], T["wins%d" % t]
-        wait(X, "uq")
+        nc, ns = T["winc%d" % (t + 1)], T["wins%d" % (t + 1)]
         if t == 0:
+            wait(X, "uq")
             wait(X, "xq")
         wait(X, "arr%d" % t)
-        a = K + NB - 128
         bank = 512 * (t % 2)
-        up(X.matmul_mx(T.psc[:, bank:bank + 128], T.uqc[:, :], T.uqs[:, :], wc[:, a:K + NB], ws[:, a:K + NB], True, True), "sco%d" % t)
+        up(X.matmul_mx(T.psc[:, bank:bank + 128], T.uqc[:, :], T.uqs[:, :], wc[:, 0:128], ws[:, 0:128], True, True), "sco%d" % t)
         wait(S, "sco%d" % t)
-        up(S.activation(T.sg[:, NB * t:NB * t + NB], T.psc[:, bank + 128 - NB:bank + 128], AF.Sign, bias=1e-30, accum_out=T.cnt[:, t:t + 1]), "act%d" % t)
+        up(S.activation(T.sg[:, NB * t:NB * t + NB], T.psc[:, bank:bank + NB], AF.Sign, bias=-1e-30, scale=-1.0, accum_out=T.cnt[:, t:t + 1]), "act%d" % t)
         vw()
         wait(V, "act%d" % t)
-        v(V.tensor_scalar(T.mn[:, q:q + n], T.nh[:, q:q + n], T.cnt[:, t:t + 1], None, AL.min))
+        v(V.tensor_scalar(T.mn[:, q:q + n], T.nh[:, q:q + n], T.cnt[:, t:t + 1], None, AL.max))
         vw()
-        v(V.tensor_tensor(T.mx[:, q:q + n], T.mn[:, q:q + n], T.bh[:, q:q + n], AL.max))
+        v(V.tensor_tensor(T.mx[:, q:q + n], T.mn[:, q:q + n], T.bh[:, q:q + n], AL.min))
         vw()
         if not last:
-            v(V.tensor_scalar(T.off[:, z + KC + 1:z + KC + 2 + LC - 1], T.mx[:, q + KC + 1:q + NL], T.hh[:, t:t + 1], 512.0, AL.subtract, AL.mult), "ofr%d" % t) if False else None
-            v(V.tensor_scalar(T.off[:, z + KC:z + KC + LC], T.mx[:, q + KC + 1:q + NL], T.hh[:, t:t + 1], 512.0, AL.subtract, AL.mult), "ofr%d" % t)
+            v(V.tensor_scalar(T.off[:, z + KC:z + NL], T.mx[:, q + KC:q + NL], T.hh[:, t:t + 1], 512.0, AL.add, AL.mult), "ofr%d" % t)
             wait(V, "ofr%d" % t)
-            oc = T.off[:, z + KC:z + KC + LC]
-            v(V.tensor_copy(T["sndc%d" % (t + 1)][:, :].bitcast(dt.uint32), wc[:, 0:K + NB].bitcast(dt.uint32).indirect(oc)), "pc%d" % (t + 1))
+            oc = T.off[:, z + KC:z + NL]
+            v(V.tensor_copy(T["sndc%d" % (t + 1)][:, :].bitcast(dt.uint32), wc[:, :].bitcast(dt.uint32).indirect(oc)), "pc%d" % (t + 1))
             wait(S, "ofr%d" % t)
-            up(S.activation(T["snds%d" % (t + 1)][:, :], ws[:, 0:K + NB].indirect(oc), AF.Copy), "ps%d" % (t + 1))
+            up(S.activation(T["snds%d" % (t + 1)][:, :], ws[:, :].indirect(oc), AF.Copy), "ps%d" % (t + 1))
             send(t + 1)
-        v(V.tensor_scalar(T.off[:, z:z + KC], T.mx[:, q:q + KC], T.hh[:, t:t + 1], 512.0, AL.subtract, AL.mult), "ew%d" % t)
+        v(V.tensor_scalar(T.off[:, z:z + KC], T.mx[:, q:q + KC], T.hh[:, t:t + 1], 512.0, AL.add, AL.mult), "ew%d" % t)
         wait(V, "ew%d" % t)
         wait(S, "ew%d" % t)
+        if last:
+            break
         oc = T.off[:, z:z + KC]
-        nc, ns = T["winc%d" % (t + 1)], T["wins%d" % (t + 1)]
-        v(V.tensor_copy(nc[:, 0:K].bitcast(dt.uint32), wc[:, 0:K + NB].bitcast(dt.uint32).indirect(oc)), "tc%d" % t)
-        up(S.activation(ns[:, 0:K], ws[:, 0:K + NB].indirect(oc), AF.Copy), "ts%d" % t)
-        if not last:
-            lists(t + 1)
-        for k in ((0,), (1, 2), (3,), (4,), ())[t]:
-            quantize_w(k)
+        v(V.tensor_copy(nc[:, NB:WIN].bitcast(dt.uint32), wc[:, :].bitcast(dt.uint32).indirect(oc)), "tc%d" % t)
+        up(S.activation(ns[:, NB:WIN], ws[:, :].indirect(oc), AF.Copy), "ts%d" % t)
+        lists_begin(t + 1)
+        quantize_w(t)
+        if t == R - 2:
+            quantize_w(t + 1)
+        lists_end(t + 1)
         wait(X, "tc%d" % t)
         wait(X, "ts%d" % t)
         wait(X, "wq%d" % t)
@@ -290,29 +275,46 @@ def rank_program(g, core, T, topo):
             wait(X, "ev%d" % (t - 3))
         for o in range(O):
             i = O * t + o
-            p = 512 * (i % 6)
-            up(X.matmul_mx(T.psy[:, p:p + K], T.wqc[:, 128 * i:128 * i + 128], T.wqs[:, 128 * i:128 * i + 128], nc[:, 0:K], ns[:, 0:K], True, True), "ym%d" % t)
+            product(i, i % 6, (0, K), (nc, ns), "ym%d" % t)
         wait(S, "ym%d" % t)
         for o in range(O):
             i = O * t + o
-            p = 512 * (i % 6)
-            if last and o == 1:
-                wait(V, "ym%d" % t)
-                v(V.tensor_copy(T.ysb[:, K * i:K * i + K], T.psy[:, p:p + K]))
+            up(S.activation(T.ysb[:, K * i:K * i + K], T.psy[:, 512 * (i % 6):512 * (i % 6) + K], AF.Copy), "ev%d" % t)
+        wait(Y, "snt%d" % (t + 1))
+        if t + 2 < R:
+            load_w(t + 2)
+        wait(Y, "ev%d" % t)
+        up(Y.dma_start(T.y[:, O * K * t:O * K * (t + 1)], T.ysb[:, O * K * t:O * K * (t + 1)]), "yl", 16)
+
+    t = R - 1
+    for h in range(2):
+        oc = T.off[:, 32 * t + KC // 2 * h:32 * t + KC // 2 * (h + 1)]
+        at = slice(NB + HK * h, NB + HK * h + HK)
+        v(V.tensor_copy(nc[:, at].bitcast(dt.uint32), wc[:, :].bitcast(dt.uint32).indirect(oc)), "lc%d" % h)
+        up(S.activation(ns[:, at], ws[:, :].indirect(oc), AF.Copy), "ls%d" % h)
+    wait(X, "wq%d" % t)
+    wait(X, "ev1")
+    wait(X, "ev2")
+    for h in range(2):
+        wait(X, "lc%d" % h)
+        wait(X, "ls%d" % h)
+        for o in range(O):
+            product(O * t + o, 2 + 2 * h + o, (HK * h, HK * h + HK), (nc, ns), "lm%d%d" % (h, o))
+    for h in range(2):
+        for o in range(O):
+            p = 512 * (2 + 2 * h + o)
+            c = K * (O * t + o) + HK * h
+            wait(V if o else S, "lm%d%d" % (h, o))
+            if o:
+                v(V.tensor_copy(T.ysb[:, c:c + HK], T.psy[:, p:p + HK]), "le%d%d" % (h, o))
             else:
-                up(S.activation(T.ysb[:, K * i:K * i + K], T.psy[:, p:p + K], AF.Copy), "ev%d" % t)
-        if not last:
-            wait(Y, "snt%d" % (t + 1))
-            if t == 0:
-                load_w(3)
-                load_w(4)
-            wait(Y, "ev%d" % t)
-            up(Y.dma_start(T.y[:, O * K * t:O * K * (t + 1)], T.ysb[:, O * K * t:O * K * (t + 1)]), "yl", 16)
-        else:
-            wait(Y, "vq")
-            up(Y.dma_start(T.y[:, K * (2 * t + 1):K * (2 * t + 2)], T.ysb[:, K * (2 * t + 1):K * (2 * t + 2)]), "yl", 16)
-            wait(S, "ev%d" % t)
-            up(S.dma_start(T.y[:, K * 2 * t:K * (2 * t + 1)], T.ysb[:, K * 2 * t:K * (2 * t + 1)]), "kq", 16)
+                up(S.activation(T.ysb[:, c:c + HK], T.psy[:, p:p + HK], AF.Copy), "le%d%d" % (h, o))
+    for h in range(2):
+        for o in range(O):
+            c = K * (O * t + o) + HK * h
+            on = S if h == 1 and o == 0 else Y
+            wait(on, "le%d%d" % (h, o))
+            up(on.dma_start(T.y[:, c:c + HK], T.ysb[:, c:c + HK]), "kq" if on is S else "yl", 16)
     for name in total:
         if waited.get(name, 0) < total[name]:
             wait(Y, name)

@@ -5,31 +5,31 @@ N, K, B, R, O = 4, 256, 32, 5, 2
 NB = (N - 1) * B
 LC = NB // 16
 KC = K // 16
-ZW = 32
 TW = 2 * K
 GW = 2 * NB
-LW = ZW + TW + GW
+LW = TW + GW
 NL = KC + LC
 HK = K // 2
 WIN = NB + K
-RL = R * LC
+BW = 4 * LC
+PW = 2 * KC
 
 SCRATCH = {
     "psc": ("psum", [128, 1024], "float32"),
     "psy": ("psum", [128, 3072], "float32"),
+    "ci": ("sbuf", [128, 2 * R, 8], "int32"), "cc": ("sbuf", [128, 2 * R, LC], "int32"), "ch": ("sbuf", [128, 2 * R, LC], "int32"),
+    "cp": ("sbuf", [128, 2 * R, LC], "float32"), "bun": ("sbuf", [128, R, BW], "uint16"),
 }
 for _n, _w, _d in (
-        ("xt", 4 * K, "bfloat16"), ("ut", 16, "bfloat16"), ("ur", 512, "bfloat16"), ("uqc", 128, "float8_e4m3fn_x4"), ("uqs", 128, "uint8"),
+        ("xt", 4 * K, "bfloat16"), ("ut", 16, "bfloat16"), ("ur", 512, "bfloat16"), ("zt", 128, "bfloat16"),
+        ("uqc", 128, "float8_e4m3fn_x4"), ("uqs", 128, "uint8"),
         ("wt", 512 * R * O, "bfloat16"), ("wqc", 128 * R * O, "float8_e4m3fn_x4"), ("wqs", 128 * R * O, "uint8"),
-        ("csi", 8 * R, "int32"), ("cdi", 8 * R, "int32"), ("csc", RL, "int32"), ("cdc", RL, "int32"), ("csh", RL, "int32"), ("cdh", RL, "int32"),
-        ("csp", RL, "float32"), ("cdp", RL, "float32"), ("bun", 4 * RL, "uint16"), ("of0", LC, "uint16"),
-        ("thr1", 16, "int32"), ("thb", 16, "int32"), ("hh", 16, "float32"), ("hn", 16, "float32"), ("hb", 16, "float32"),
-        ("pidx", 32, "int32"), ("p3i", 32, "int32"), ("u3", 32, "uint16"),
-        ("p15i", 1, "int32"), ("oddi", 1, "int32"), ("p15f", 1, "float32"), ("oddf", 1, "float32"), ("odd16", 1, "float32"), ("evf", 1, "float32"),
-        ("zodd", 1, "float32"), ("zev", 1, "float32"), ("k16", KC, "float32"), ("keyb", KC, "float32"), ("jval", NB, "bfloat16"),
-        ("lb", R * LW, "bfloat16"), ("tb", R * 32 * NL, "bfloat16"), ("lv", R * NL, "float32"),
-        ("nh", R * NL, "float32"), ("bh", R * NL, "float32"), ("mn", R * NL, "float32"), ("mx", R * NL, "float32"),
-        ("off", R * 32, "uint16"), ("sg", R * NB, "float32"), ("cnt", R, "float32"), ("ysb", R * O * K, "float32")):
+        ("of0", LC, "uint16"), ("thr1", 16, "int32"), ("thb", 16, "int32"),
+        ("pidx", KC, "int32"), ("p15", KC, "int32"), ("k16", KC, "int32"), ("oddi", 1, "int32"), ("odd16", 1, "float32"),
+        ("pe0", 1, "float32"), ("pe1", 1, "float32"), ("base", 2 * R, "float32"), ("jval", NB, "bfloat16"),
+        ("lb", R * LW, "bfloat16"), ("tb", R * 32 * NL, "bfloat16"), ("lv", R * NL, "float32"), ("lw", PW + 16 * R, "float32"),
+        ("idx", 4 * R, "uint16"), ("offs", 16 * R, "uint16"), ("offt", 16 * R, "uint16"),
+        ("sg", R * NB, "float32"), ("cnt", R, "float32"), ("ysb", R * O * K, "float32")):
     SCRATCH[_n] = ("sbuf", [128, _w], _d)
 for _t in range(R):
     SCRATCH["sndc%d" % _t] = ("sbuf", [128, NB], "float8_e4m3fn_x4")
@@ -38,9 +38,9 @@ for _t in range(R + 1):
     SCRATCH["winc%d" % _t] = ("sbuf", [128, WIN], "float8_e4m3fn_x4")
     SCRATCH["wins%d" % _t] = ("sbuf", [128, WIN], "uint8")
 
-SEMAPHORES = ["xl", "csl", "cdl", "ul", "thl", "iot", "tbc", "u3r", "urr", "uq", "xq", "o0", "vq", "kq", "yl"]
+SEMAPHORES = ["xl", "csl", "cdl", "ul", "thl", "iot", "tbc", "ztr", "urr", "uq", "xq", "o0", "vq", "kq", "yl"]
 for _t in range(R):
-    SEMAPHORES += ["%s%d" % (n, _t) for n in ("arr", "snt", "pc", "ps", "tc", "ts", "sco", "act", "ofr", "wl", "wq", "ym", "ev", "ew", "sc", "gt")]
+    SEMAPHORES += ["%s%d" % (n, _t) for n in ("arr", "snt", "pc", "ps", "tc", "ts", "sco", "act", "ofr", "wl", "wq", "ym", "ev", "ew", "sc", "gt", "fl")]
 SEMAPHORES += ["%s%d%d" % (n, h, o) for n in ("lm", "le") for h in range(2) for o in range(O)] + ["lc0", "lc1", "ls0", "ls1"]
 
 AL = AluOpType
@@ -70,58 +70,57 @@ def rank_program(g, core, T, topo):
     def vw():
         wait(V, "vq")
 
-    up(Y.dma_start(T.xt[:, :], T.x[:, :]), "xl", 16)
-    up(S.dma_start(T.csi[0:16, :], T.cs[:, :]), "csl", 16)
-    up(S.dma_start(T.csi[16:32, :], T.cs[:, :]), "csl", 16)
-    up(S.dma_start(T.thr1[0:1, :], T.thr[:, :]), "thl", 16)
-    up(Y.dma_start(T.ut[:, :], T.u[:, 0:16]), "ul", 16)
-    up(Y.dma_start(T.cdi[0:16, :], T.cd[:, :]), "cdl", 16)
-    up(Y.dma_start(T.cdi[16:32, :], T.cd[:, :]), "cdl", 16)
+    def load_w(t):
+        up(Y.dma_start(T.wt[:, 1024 * t:1024 * t + 1024], T.w[:, 1024 * t:1024 * t + 1024]), "wl%d" % t, 16)
 
-    up(g.iota(T.pidx[:, :], [[0, 32]], 0, 1), "iot")
-    up(g.iota(T.k16[:, :], [[16, KC]], 0, 0, allow_small_or_imprecise_dtypes=True), "iot")
+    def store_y(t):
+        wait(Y, "ev%d" % t)
+        up(Y.dma_start(T.y[:, O * K * t:O * K * (t + 1)], T.ysb[:, O * K * t:O * K * (t + 1)]), "yl", 16)
+
+    BETWEEN = ((("w", 2),), (("w", 3),), (("w", 4), ("y", 0)), (("y", 1),), (("y", 2), ("y", 3)))
+
+    def between(t):
+        wait(Y, "snt%d" % t)
+        for kind, i in BETWEEN[t]:
+            (load_w if kind == "w" else store_y)(i)
+
+    up(Y.dma_start(T.ci[0:16, 0:R, :], T.cs[:, :]), "csl", 16)
+    up(S.dma_start(T.ci[16:32, 0:R, :], T.cs[:, :]), "csl", 16)
+    up(Y.dma_start(T.xt[:, :], T.x[:, :]), "xl", 16)
+    up(S.dma_start(T.ci[0:16, R:2 * R, :], T.cd[:, :]), "cdl", 16)
+    up(S.dma_start(T.ci[16:32, R:2 * R, :], T.cd[:, :]), "cdl", 16)
+    up(Y.dma_start(T.ut[:, :], T.u[:, 0:16]), "ul", 16)
+    up(Y.dma_start(T.thr1[0:1, :], T.thr[:, :]), "thl", 16)
+    load_w(0)
+    load_w(1)
+
+    up(g.iota(T.pidx[:, :], [[0, KC]], 0, 1), "iot")
+    up(g.iota(T.k16[:, :], [[16, KC]], NB, 0), "iot")
     up(g.iota(T.jval[:, :], [[1, NB]], 0, 0, allow_small_or_imprecise_dtypes=True), "iot")
 
-    def fill(t):
-        v(V.memset(T.lb[:, LW * t:LW * t + ZW + TW], 512.0))
-
-    fill(0)
+    v(V.memset(T.lb[:, 0:TW], 512.0), "fl0")
+    v(V.memset(T.zt[:, :], 0.0), "ztr")
     wait(V, "iot")
-    v(V.tensor_scalar(T.p3i[:, :], T.pidx[:, :], 3, None, AL.bitwise_and))
-    v(V.tensor_scalar(T.p15i[:, :], T.pidx[:, 0:1], 15, None, AL.bitwise_and))
-    v(V.tensor_scalar(T.oddi[:, :], T.pidx[:, 0:1], 4, 1, AL.logical_shift_right, AL.bitwise_and))
+    v(V.tensor_scalar(T.p15[:, :], T.pidx[:, :], 15, None, AL.bitwise_and))
+    v(V.tensor_scalar(T.oddi[:, :], T.pidx[:, 0:1], 16, None, AL.bitwise_and))
     vw()
-    v(V.tensor_copy(T.u3[:, :], T.p3i[:, :]), "u3r")
-    v(V.tensor_copy(T.p15f[:, :], T.p15i[:, :]))
-    v(V.tensor_copy(T.oddf[:, :], T.oddi[:, :]))
-    vw()
-    v(V.tensor_scalar(T.keyb[:, :], T.k16[:, :], T.p15f[:, 0:1], None, AL.add))
-    v(V.tensor_scalar(T.odd16[:, :], T.oddf[:, :], 16.0, None, AL.mult))
-    v(V.tensor_scalar(T.evf[:, :], T.oddf[:, :], -1.0, 1.0, AL.mult, AL.add))
-    v(V.tensor_scalar(T.zodd[:, :], T.oddf[:, :], float(16 + ZW), None, AL.mult))
-    v(V.tensor_scalar(T.zev[:, :], T.oddf[:, :], float(-ZW), float(ZW), AL.mult, AL.add))
-    for t in range(1, R):
-        fill(t)
-
-    wait(g, "thl")
-    up(g.partition_broadcast(T.thb[:, :], T.thr1[0:1, :], 128), "tbc")
+    v(V.tensor_tensor(T.lw[:, 0:PW:2], T.p15[:, :], T.k16[:, :], AL.add))
+    v(V.tensor_copy(T.odd16[:, :], T.oddi[:, :]))
+    v(V.tensor_scalar(T.pe0[:, :], T.p15[:, 0:1], 1024.0, 256.0 + NB + 1, AL.mult, AL.add))
 
     runs = []
     if r > 0:
         runs.append((0, 0, 2 * r))
     if r < N - 1:
         runs.append((2 * r + 2, 2 * r, LC - 2 * r))
-
-    def compact(dst, src):
-        for a, b, n in runs:
-            for i in range(n):
-                v(V.tensor_copy(T[dst][0:32, b + i:RL:LC], T[src][0:32, a + i:8 * R:8]))
+    q0 = slice(0, 32)
 
     wait(V, "csl")
-    for k in range(0, 128, 32):
-        for a, b, n in runs:
-            v(V.tensor_copy(T.of0[k:k + 32, b:b + n], T.csi[0:32, a:a + n]), "o0")
-    compact("csc", "csi")
+    for a, b, n in runs:
+        v(V.tensor_copy(T.of0[q0, b:b + n], T.ci[q0, 0, a:a + n]), "o0")
+    wait(V, "o0")
+    for k in (32, 64, 96):
+        v(V.tensor_copy(T.of0[k:k + 32, :], T.of0[q0, :]), "o0")
     wait(V, "xl")
     v(V.quantize_mx(T.winc0[:, NB:WIN], T.wins0[:, NB:WIN], T.xt[:, :]), "xq")
     wait(V, "o0")
@@ -143,7 +142,7 @@ def rank_program(g, core, T, topo):
         return RemoteDMATransfer(dst_ids=[DstId(rid=rid, pnc=pid)], dma_engine_mask=sum(1 << e for e in topo.engines(core, to)[first:first + n]),
                                  remote_sem=T.sem["arr%d" % t], srcs=[src], dsts=[dst])
 
-    PLAN = (("c", ((0, 0, 2), (1, 2, 2), (2, 4, 2))), ("s", ((0, 6, 2),)), ("s", ((1, 0, 4), (2, 4, 4))))
+    PLAN = (("c", ((0, 0, 4), (1, 4, 2), (2, 6, 2))), ("s", ((0, 0, 2), (1, 2, 2), (2, 4, 4))))
 
     def send(t):
         n = 0
@@ -154,44 +153,46 @@ def rank_program(g, core, T, topo):
         total["snt%d" % t] = n
         total["arr%d" % t] = sum(p[2] for s in others for _, tr in PLAN for p in tr if [d for d in range(N) if d != s][p[0]] == r)
 
+    def fill(t):
+        up(g.iota(T.lb[:, LW * t:LW * t + TW], [[0, TW]], 512, 0, allow_small_or_imprecise_dtypes=True), "fl%d" % t)
+
     send(0)
 
-    wait(S, "u3r")
-    wait(S, "ul")
-    up(S.activation(T.ur[:, :], T.ut[:, :].indirect(T.u3[:, :]), AF.Copy), "urr")
+    wait(g, "thl")
+    up(g.partition_broadcast(T.thb[:, :], T.thr1[0:1, :], 128), "tbc")
+    fill(1)
 
-    q0 = slice(0, 32)
+    wait(S, "ul")
+    wait(S, "ztr")
+    for i in range(4):
+        up(S.activation(T.ur[:, i:512:4], T.zt[:, :], AF.Identity, bias=T.ut[:, i:i + 1]), "urr")
+
     wait(V, "cdl")
-    compact("cdc", "cdi")
+    for a, b, n in runs:
+        v(V.tensor_copy(T.cc[q0, :, b:b + n], T.ci[q0, :, a:a + n]))
     vw()
-    v(V.tensor_scalar(T.cdh[q0, :], T.cdc[q0, :], 240, None, AL.bitwise_and))
-    v(V.tensor_scalar(T.csh[q0, :], T.csc[q0, :], 240, None, AL.bitwise_and))
-    v(V.tensor_copy(T.bun[q0, 3 * RL:4 * RL], T.csc[q0, :]))
+    v(V.tensor_scalar(T.ch[q0, :, :], T.cc[q0, :, :], 240, None, AL.bitwise_and))
+    v(V.tensor_copy(T.bun[q0, :, 3 * LC:BW], T.cc[q0, 0:R, :]))
     vw()
-    v(V.tensor_tensor(T.cdp[q0, :], T.cdc[q0, :], T.cdh[q0, :], AL.add))
-    v(V.tensor_tensor(T.csp[q0, :], T.csc[q0, :], T.csh[q0, :], AL.add))
+    v(V.tensor_tensor(T.cp[q0, :, :], T.cc[q0, :, :], T.ch[q0, :, :], AL.add))
     vw()
-    v(V.tensor_scalar(T.bun[q0, 0:RL], T.cdp[q0, :], T.odd16[q0, 0:1], None, AL.add))
-    v(V.tensor_scalar(T.bun[q0, RL:3 * RL:2], T.csp[q0, :], T.evf[q0, 0:1], T.zev[q0, 0:1], AL.mult, AL.add))
-    v(V.tensor_scalar(T.bun[q0, RL + 1:3 * RL:2], T.csp[q0, :], T.oddf[q0, 0:1], T.zodd[q0, 0:1], AL.mult, AL.add))
+    v(V.tensor_scalar(T.bun[q0, :, 0:LC], T.cp[q0, R:2 * R, :], T.odd16[q0, 0:1], None, AL.add))
+    for i in range(2):
+        v(V.tensor_scalar(T.bun[q0, :, LC + i:3 * LC:2], T.cp[q0, 0:R, :], T.odd16[q0, 0:1], None, AL.add))
     vw()
     for k in (32, 64, 96):
-        v(V.tensor_copy(T.bun[k:k + 32, :], T.bun[q0, :]))
-    wait(V, "tbc")
-    v(V.tensor_scalar(T.hh[:, :], T.thb[:, :], 2.0, float(-NB - 1), AL.mult, AL.add))
-    v(V.tensor_scalar(T.hn[:, :], T.thb[:, :], -2.0, float(NB), AL.mult, AL.add))
-    v(V.tensor_scalar(T.hb[:, :], T.thb[:, :], -2.0, NB + 1 + NB / 512.0, AL.mult, AL.add))
+        v(V.tensor_copy(T.bun[k:k + 32, :, :], T.bun[q0, :, :]))
 
     def lists_begin(t):
-        z, q = LW * t, NL * t
+        z = LW * t
+        wait(V, "fl%d" % t)
         vw()
-        v(V.tensor_copy(T.lb[:, z + ZW:z + ZW + TW].indirect(T.bun[:, LC * t:LC * t + LC]), T.jval[:, :]), "sc%d" % t)
-        h = T.hb[:, t:t + 1]
-        v(V.tensor_scalar(T.bh[:, q:q + KC], T.keyb[:, :], 1.0 / 512, h, AL.mult, AL.add))
+        v(V.tensor_copy(T.lb[:, z:z + TW].indirect(T.bun[:, t, 0:LC]), T.jval[:, :]), "sc%d" % t)
         if t + 1 < R:
-            v(V.tensor_scalar(T.bh[:, q + KC:q + NL], T.bun[:, 3 * RL + LC * (t + 1):3 * RL + LC * (t + 2)], 1.0 / 512, h, AL.mult, AL.add))
+            p = PW + 16 * t
+            v(V.tensor_scalar(T.lw[:, p:p + 2 * LC:2], T.bun[:, t + 1, 3 * LC:BW], float(NB), None, AL.add))
             wait(S, "sc%d" % t)
-            up(S.activation(T.lb[:, z + ZW + TW:z + LW], T.lb[:, z:z + ZW + TW].indirect(T.bun[:, RL + 2 * LC * (t + 1):RL + 2 * LC * (t + 2)]), AF.Copy), "gt%d" % t)
+            up(S.activation(T.lb[:, z + TW:z + LW], T.lb[:, z:z + TW].indirect(T.bun[:, t + 1, LC:3 * LC]), AF.Copy), "gt%d" % t)
 
     def lists_end(t):
         z, q, y = LW * t, NL * t, 32 * NL * t
@@ -199,19 +200,24 @@ def rank_program(g, core, T, topo):
         wait(V, "sc%d" % t)
         if t + 1 < R:
             wait(V, "gt%d" % t)
-        v(V.transpose(T.tb[:, y:y + 32 * n], T.lb[:, z + ZW:z + ZW + 32 * n]))
+        v(V.transpose(T.tb[:, y:y + 32 * n], T.lb[:, z:z + 32 * n]))
         vw()
-        v(V.tensor_tensor(T.lv[:, q:q + n], T.tb[:, y:y + 32 * n:32], T.tb[:, y + 16:y + 32 * n:32], AL.add))
+        v(V.tensor_tensor(T.lv[:, q:q + n], T.tb[:, y:y + 32 * n:32], T.tb[:, y + 16:y + 32 * n:32], AL.min))
         vw()
-        v(V.tensor_scalar(T.nh[:, q:q + n], T.lv[:, q:q + n], 1.0 / 512, T.hn[:, t:t + 1], AL.mult, AL.add))
+        v(V.tensor_tensor(T.lw[:, 1:PW:2], T.lv[:, q:q + KC], T.lw[:, 0:PW:2], AL.min))
+        if t + 1 < R:
+            p = PW + 16 * t
+            v(V.tensor_tensor(T.lw[:, p + 1:p + 2 * LC:2], T.lv[:, q + KC:q + NL], T.lw[:, p:p + 2 * LC:2], AL.min))
 
     lists_begin(0)
+    v(V.tensor_scalar(T.pe1[:, :], T.pe0[:, :], 1024.0 * (LC - 1) + 256.0 + NB + 1, None, AL.min))
+    wait(V, "tbc")
+    vw()
+    v(V.tensor_scalar(T.base[:, 0:R], T.thb[:, 0:R], -2.0, T.pe0[:, 0:1], AL.mult, AL.add))
+    v(V.tensor_scalar(T.base[:, R:2 * R], T.thb[:, 0:R], -2.0, T.pe1[:, 0:1], AL.mult, AL.add))
     wait(V, "urr")
     v(V.quantize_mx(T.uqc[:, :], T.uqs[:, :], T.ur[:, :]), "uq")
     lists_end(0)
-
-    def load_w(t):
-        up(Y.dma_start(T.wt[:, 1024 * t:1024 * t + 1024], T.w[:, 1024 * t:1024 * t + 1024]), "wl%d" % t, 16)
 
     def quantize_w(t):
         wait(V, "wl%d" % t)
@@ -223,14 +229,10 @@ def rank_program(g, core, T, topo):
         a, b = NB + cols[0], NB + cols[1]
         up(X.matmul_mx(T.psy[:, p:p + b - a], T.wqc[:, 128 * i:128 * i + 128], T.wqs[:, 128 * i:128 * i + 128], win[0][:, a:b], win[1][:, a:b], True, True), name)
 
-    wait(Y, "snt0")
-    load_w(0)
-    load_w(1)
+    between(0)
 
     for t in range(R):
         last = t + 1 == R
-        q, z = NL * t, 32 * t
-        n = KC if last else NL
         wc, ws = T["winc%d" % t], T["wins%d" % t]
         nc, ns = T["winc%d" % (t + 1)], T["wins%d" % (t + 1)]
         if t == 0:
@@ -243,24 +245,24 @@ def rank_program(g, core, T, topo):
         up(S.activation(T.sg[:, NB * t:NB * t + NB], T.psc[:, bank:bank + NB], AF.Sign, bias=-1e-30, scale=-1.0, accum_out=T.cnt[:, t:t + 1]), "act%d" % t)
         vw()
         wait(V, "act%d" % t)
-        v(V.tensor_scalar(T.mn[:, q:q + n], T.nh[:, q:q + n], T.cnt[:, t:t + 1], None, AL.max))
-        vw()
-        v(V.tensor_tensor(T.mx[:, q:q + n], T.mn[:, q:q + n], T.bh[:, q:q + n], AL.min))
+        v(V.tensor_scalar(T.idx[:, 4 * t:4 * t + 4:2], T.base[:, t:2 * R:R], T.cnt[:, t:t + 1], 1.0 / 512, AL.subtract, AL.mult))
         vw()
         if not last:
-            v(V.tensor_scalar(T.off[:, z + KC:z + NL], T.mx[:, q + KC:q + NL], T.hh[:, t:t + 1], 512.0, AL.add, AL.mult), "ofr%d" % t)
+            v(V.tensor_copy(T.offs[:, 16 * t:16 * t + 16], T.lw[:, PW + 16 * t:PW + 16 * t + 2 * LC].indirect(T.idx[:, 4 * t + 2:4 * t + 3])), "ofr%d" % t)
             wait(V, "ofr%d" % t)
-            oc = T.off[:, z + KC:z + NL]
+            oc = T.offs[:, 16 * t:16 * t + LC]
             v(V.tensor_copy(T["sndc%d" % (t + 1)][:, :].bitcast(dt.uint32), wc[:, :].bitcast(dt.uint32).indirect(oc)), "pc%d" % (t + 1))
             wait(S, "ofr%d" % t)
             up(S.activation(T["snds%d" % (t + 1)][:, :], ws[:, :].indirect(oc), AF.Copy), "ps%d" % (t + 1))
             send(t + 1)
-        v(V.tensor_scalar(T.off[:, z:z + KC], T.mx[:, q:q + KC], T.hh[:, t:t + 1], 512.0, AL.add, AL.mult), "ew%d" % t)
+            if t + 2 < R:
+                fill(t + 2)
+        v(V.tensor_copy(T.offt[:, 16 * t:16 * t + 16], T.lw[:, 0:PW].indirect(T.idx[:, 4 * t:4 * t + 1])), "ew%d" % t)
         wait(V, "ew%d" % t)
         wait(S, "ew%d" % t)
         if last:
             break
-        oc = T.off[:, z:z + KC]
+        oc = T.offt[:, 16 * t:16 * t + KC]
         v(V.tensor_copy(nc[:, NB:WIN].bitcast(dt.uint32), wc[:, :].bitcast(dt.uint32).indirect(oc)), "tc%d" % t)
         up(S.activation(ns[:, NB:WIN], ws[:, :].indirect(oc), AF.Copy), "ts%d" % t)
         lists_begin(t + 1)
@@ -280,15 +282,11 @@ def rank_program(g, core, T, topo):
         for o in range(O):
             i = O * t + o
             up(S.activation(T.ysb[:, K * i:K * i + K], T.psy[:, 512 * (i % 6):512 * (i % 6) + K], AF.Copy), "ev%d" % t)
-        wait(Y, "snt%d" % (t + 1))
-        if t + 2 < R:
-            load_w(t + 2)
-        wait(Y, "ev%d" % t)
-        up(Y.dma_start(T.y[:, O * K * t:O * K * (t + 1)], T.ysb[:, O * K * t:O * K * (t + 1)]), "yl", 16)
+        between(t + 1)
 
     t = R - 1
     for h in range(2):
-        oc = T.off[:, 32 * t + KC // 2 * h:32 * t + KC // 2 * (h + 1)]
+        oc = T.offt[:, 16 * t + KC // 2 * h:16 * t + KC // 2 * (h + 1)]
         at = slice(NB + HK * h, NB + HK * h + HK)
         v(V.tensor_copy(nc[:, at].bitcast(dt.uint32), wc[:, :].bitcast(dt.uint32).indirect(oc)), "lc%d" % h)
         up(S.activation(ns[:, at], ws[:, :].indirect(oc), AF.Copy), "ls%d" % h)

from concourse.bass import DstId, RemoteDMATransfer
from concourse.mybir import dt, AluOpType, ActivationFunctionType

N, K, B, R, O = 4, 256, 32, 5, 2
NB = (N - 1) * B
LC = NB // 16
KC = K // 16
TW = 2 * K
GW = 2 * NB
LW = TW + GW
NL = KC + LC
HK = K // 2
WIN = NB + K
BW = 4 * LC
PW = 2 * KC

SCRATCH = {
    "psc": ("psum", [128, 1024], "float32"),
    "psy": ("psum", [128, 3072], "float32"),
    "ci": ("sbuf", [128, 2 * R, 8], "int32"), "cc": ("sbuf", [128, 2 * R, LC], "int32"), "ch": ("sbuf", [128, 2 * R, LC], "int32"),
    "cp": ("sbuf", [128, 2 * R, LC], "float32"), "bun": ("sbuf", [128, R, BW], "uint16"),
}
for _n, _w, _d in (
        ("xt", 4 * K, "bfloat16"), ("ut", 16, "bfloat16"), ("ur", 512, "bfloat16"), ("zt", 128, "bfloat16"),
        ("uqc", 128, "float8_e4m3fn_x4"), ("uqs", 128, "uint8"),
        ("wt", 512 * R * O, "bfloat16"), ("wqc", 128 * R * O, "float8_e4m3fn_x4"), ("wqs", 128 * R * O, "uint8"),
        ("of0", LC, "uint16"), ("thr1", 16, "int32"), ("thb", 16, "int32"),
        ("pidx", KC, "int32"), ("p15", KC, "int32"), ("k16", KC, "int32"), ("oddi", 1, "int32"), ("odd16", 1, "float32"),
        ("pe0", 1, "float32"), ("pe1", 1, "float32"), ("base", 2 * R, "float32"), ("jval", NB, "bfloat16"),
        ("lb", R * LW, "bfloat16"), ("tb", R * 32 * NL, "bfloat16"), ("lv", R * NL, "float32"), ("lw", PW + 16 * R, "float32"),
        ("idx", 4 * R, "uint16"), ("offs", 16 * R, "uint16"), ("offt", 16 * R, "uint16"),
        ("sg", R * NB, "float32"), ("cnt", R, "float32"), ("ysb", R * O * K, "float32")):
    SCRATCH[_n] = ("sbuf", [128, _w], _d)
for _t in range(R):
    SCRATCH["sndc%d" % _t] = ("sbuf", [128, NB], "float8_e4m3fn_x4")
    SCRATCH["snds%d" % _t] = ("sbuf", [128, NB], "uint8")
for _t in range(R + 1):
    SCRATCH["winc%d" % _t] = ("sbuf", [128, WIN], "float8_e4m3fn_x4")
    SCRATCH["wins%d" % _t] = ("sbuf", [128, WIN], "uint8")

SEMAPHORES = ["xl", "csl", "cdl", "ul", "thl", "iot", "tbc", "ztr", "urr", "uq", "xq", "o0", "vq", "kq", "yl"]
for _t in range(R):
    SEMAPHORES += ["%s%d" % (n, _t) for n in ("arr", "snt", "pc", "ps", "tc", "ts", "sco", "act", "ofr", "wl", "wq", "ym", "ev", "ew", "sc", "gt", "fl")]
SEMAPHORES += ["%s%d%d" % (n, h, o) for n in ("lm", "le") for h in range(2) for o in range(O)] + ["lc0", "lc1", "ls0", "ls1"]

AL = AluOpType
AF = ActivationFunctionType


def rank_program(g, core, T, topo):
    r = T.rank_of(core)
    if r is None:
        return
    others = [s for s in range(N) if s != r]
    V, S, X, Y = g.vector, g.scalar, g.tensor, g.sync
    total = {}
    waited = {}

    def up(call, name, n=1):
        call.then_inc(T.sem[name], n)
        total[name] = total.get(name, 0) + n

    def wait(q, name):
        q.wait_ge(T.sem[name], total[name])
        waited[name] = total[name]

    def v(call, name="vq"):
        up(call, name)

    def vw():
        wait(V, "vq")

    def load_w(t):
        up(Y.dma_start(T.wt[:, 1024 * t:1024 * t + 1024], T.w[:, 1024 * t:1024 * t + 1024]), "wl%d" % t, 16)

    def store_y(t):
        wait(Y, "ev%d" % t)
        up(Y.dma_start(T.y[:, O * K * t:O * K * (t + 1)], T.ysb[:, O * K * t:O * K * (t + 1)]), "yl", 16)

    BETWEEN = ((("w", 2),), (("w", 3),), (("w", 4), ("y", 0)), (("y", 1),), (("y", 2), ("y", 3)))

    def between(t):
        wait(Y, "snt%d" % t)
        for kind, i in BETWEEN[t]:
            (load_w if kind == "w" else store_y)(i)

    up(Y.dma_start(T.ci[0:16, 0:R, :], T.cs[:, :]), "csl", 16)
    up(S.dma_start(T.ci[16:32, 0:R, :], T.cs[:, :]), "csl", 16)
    up(Y.dma_start(T.xt[:, :], T.x[:, :]), "xl", 16)
    up(S.dma_start(T.ci[0:16, R:2 * R, :], T.cd[:, :]), "cdl", 16)
    up(S.dma_start(T.ci[16:32, R:2 * R, :], T.cd[:, :]), "cdl", 16)
    up(Y.dma_start(T.ut[:, :], T.u[:, 0:16]), "ul", 16)
    up(Y.dma_start(T.thr1[0:1, :], T.thr[:, :]), "thl", 16)
    load_w(0)
    load_w(1)

    up(g.iota(T.pidx[:, :], [[0, KC]], 0, 1), "iot")
    up(g.iota(T.k16[:, :], [[16, KC]], NB, 0), "iot")
    up(g.iota(T.jval[:, :], [[1, NB]], 0, 0, allow_small_or_imprecise_dtypes=True), "iot")

    v(V.memset(T.lb[:, 0:TW], 512.0), "fl0")
    v(V.memset(T.zt[:, :], 0.0), "ztr")
    wait(V, "iot")
    v(V.tensor_scalar(T.p15[:, :], T.pidx[:, :], 15, None, AL.bitwise_and))
    v(V.tensor_scalar(T.oddi[:, :], T.pidx[:, 0:1], 16, None, AL.bitwise_and))
    vw()
    v(V.tensor_tensor(T.lw[:, 0:PW:2], T.p15[:, :], T.k16[:, :], AL.add))
    v(V.tensor_copy(T.odd16[:, :], T.oddi[:, :]))
    v(V.tensor_scalar(T.pe0[:, :], T.p15[:, 0:1], 1024.0, 256.0 + NB + 1, AL.mult, AL.add))

    runs = []
    if r > 0:
        runs.append((0, 0, 2 * r))
    if r < N - 1:
        runs.append((2 * r + 2, 2 * r, LC - 2 * r))
    q0 = slice(0, 32)

    wait(V, "csl")
    for a, b, n in runs:
        v(V.tensor_copy(T.of0[q0, b:b + n], T.ci[q0, 0, a:a + n]), "o0")
    wait(V, "o0")
    for k in (32, 64, 96):
        v(V.tensor_copy(T.of0[k:k + 32, :], T.of0[q0, :]), "o0")
    wait(V, "xl")
    v(V.quantize_mx(T.winc0[:, NB:WIN], T.wins0[:, NB:WIN], T.xt[:, :]), "xq")
    wait(V, "o0")
    wait(V, "xq")
    v(V.tensor_copy(T.sndc0[:, :].bitcast(dt.uint32), T.winc0[:, NB:WIN].bitcast(dt.uint32).indirect(T.of0[:, :])), "pc0")
    wait(S, "o0")
    wait(S, "xq")
    up(S.activation(T.snds0[:, :], T.wins0[:, NB:WIN].indirect(T.of0[:, :]), AF.Copy), "ps0")

    def piece(kind, t, b, first, n):
        d = others[b]
        to = T.cores[d]
        rid, pid, _ = topo.addr(to)
        at = B * (r if r < d else r - 1)
        src = T["snd%s%d" % (kind, t)][:, B * b:B * b + B]
        dst = T["win%s%d" % (kind, t)][:, at:at + B]
        if kind == "c":
            src, dst = src.bitcast(dt.uint8), dst.bitcast(dt.uint8)
        return RemoteDMATransfer(dst_ids=[DstId(rid=rid, pnc=pid)], dma_engine_mask=sum(1 << e for e in topo.engines(core, to)[first:first + n]),
                                 remote_sem=T.sem["arr%d" % t], srcs=[src], dsts=[dst])

    PLAN = (("c", ((0, 0, 4), (1, 4, 2), (2, 6, 2))), ("s", ((0, 0, 2), (1, 2, 2), (2, 4, 4))))

    def send(t):
        n = 0
        for kind, tr in PLAN:
            wait(g, "p%s%d" % (kind, t))
            g.remote_dma_fused([piece(kind, t, *p) for p in tr], local_sem=T.sem["snt%d" % t])
            n += sum(p[2] for p in tr)
        total["snt%d" % t] = n
        total["arr%d" % t] = sum(p[2] for s in others for _, tr in PLAN for p in tr if [d for d in range(N) if d != s][p[0]] == r)

    def fill(t):
        up(g.iota(T.lb[:, LW * t:LW * t + TW], [[0, TW]], 512, 0, allow_small_or_imprecise_dtypes=True), "fl%d" % t)

    send(0)

    wait(g, "thl")
    up(g.partition_broadcast(T.thb[:, :], T.thr1[0:1, :], 128), "tbc")
    fill(1)

    wait(S, "ul")
    wait(S, "ztr")
    for i in range(4):
        up(S.activation(T.ur[:, i:512:4], T.zt[:, :], AF.Identity, bias=T.ut[:, i:i + 1]), "urr")

    wait(V, "cdl")
    for a, b, n in runs:
        v(V.tensor_copy(T.cc[q0, :, b:b + n], T.ci[q0, :, a:a + n]))
    vw()
    v(V.tensor_scalar(T.ch[q0, :, :], T.cc[q0, :, :], 240, None, AL.bitwise_and))
    v(V.tensor_copy(T.bun[q0, :, 3 * LC:BW], T.cc[q0, 0:R, :]))
    vw()
    v(V.tensor_tensor(T.cp[q0, :, :], T.cc[q0, :, :], T.ch[q0, :, :], AL.add))
    vw()
    v(V.tensor_scalar(T.bun[q0, :, 0:LC], T.cp[q0, R:2 * R, :], T.odd16[q0, 0:1], None, AL.add))
    for i in range(2):
        v(V.tensor_scalar(T.bun[q0, :, LC + i:3 * LC:2], T.cp[q0, 0:R, :], T.odd16[q0, 0:1], None, AL.add))
    vw()
    for k in (32, 64, 96):
        v(V.tensor_copy(T.bun[k:k + 32, :, :], T.bun[q0, :, :]))

    def lists_begin(t):
        z = LW * t
        wait(V, "fl%d" % t)
        vw()
        v(V.tensor_copy(T.lb[:, z:z + TW].indirect(T.bun[:, t, 0:LC]), T.jval[:, :]), "sc%d" % t)
        if t + 1 < R:
            p = PW + 16 * t
            v(V.tensor_scalar(T.lw[:, p:p + 2 * LC:2], T.bun[:, t + 1, 3 * LC:BW], float(NB), None, AL.add))
            wait(S, "sc%d" % t)
            up(S.activation(T.lb[:, z + TW:z + LW], T.lb[:, z:z + TW].indirect(T.bun[:, t + 1, LC:3 * LC]), AF.Copy), "gt%d" % t)

    def lists_end(t):
        z, q, y = LW * t, NL * t, 32 * NL * t
        n = NL if t + 1 < R else KC
        wait(V, "sc%d" % t)
        if t + 1 < R:
            wait(V, "gt%d" % t)
        v(V.transpose(T.tb[:, y:y + 32 * n], T.lb[:, z:z + 32 * n]))
        vw()
        v(V.tensor_tensor(T.lv[:, q:q + n], T.tb[:, y:y + 32 * n:32], T.tb[:, y + 16:y + 32 * n:32], AL.min))
        vw()
        v(V.tensor_tensor(T.lw[:, 1:PW:2], T.lv[:, q:q + KC], T.lw[:, 0:PW:2], AL.min))
        if t + 1 < R:
            p = PW + 16 * t
            v(V.tensor_tensor(T.lw[:, p + 1:p + 2 * LC:2], T.lv[:, q + KC:q + NL], T.lw[:, p:p + 2 * LC:2], AL.min))

    lists_begin(0)
    v(V.tensor_scalar(T.pe1[:, :], T.pe0[:, :], 1024.0 * (LC - 1) + 256.0 + NB + 1, None, AL.min))
    wait(V, "tbc")
    vw()
    v(V.tensor_scalar(T.base[:, 0:R], T.thb[:, 0:R], -2.0, T.pe0[:, 0:1], AL.mult, AL.add))
    v(V.tensor_scalar(T.base[:, R:2 * R], T.thb[:, 0:R], -2.0, T.pe1[:, 0:1], AL.mult, AL.add))
    wait(V, "urr")
    v(V.quantize_mx(T.uqc[:, :], T.uqs[:, :], T.ur[:, :]), "uq")
    lists_end(0)

    def quantize_w(t):
        wait(V, "wl%d" % t)
        for i in (2 * t, 2 * t + 1):
            v(V.quantize_mx(T.wqc[:, 128 * i:128 * i + 128], T.wqs[:, 128 * i:128 * i + 128], T.wt[:, 512 * i:512 * i + 512]), "wq%d" % t)

    def product(i, bank, cols, win, name):
        p = 512 * bank
        a, b = NB + cols[0], NB + cols[1]
        up(X.matmul_mx(T.psy[:, p:p + b - a], T.wqc[:, 128 * i:128 * i + 128], T.wqs[:, 128 * i:128 * i + 128], win[0][:, a:b], win[1][:, a:b], True, True), name)

    between(0)

    for t in range(R):
        last = t + 1 == R
        wc, ws = T["winc%d" % t], T["wins%d" % t]
        nc, ns = T["winc%d" % (t + 1)], T["wins%d" % (t + 1)]
        if t == 0:
            wait(X, "uq")
            wait(X, "xq")
        wait(X, "arr%d" % t)
        bank = 512 * (t % 2)
        up(X.matmul_mx(T.psc[:, bank:bank + 128], T.uqc[:, :], T.uqs[:, :], wc[:, 0:128], ws[:, 0:128], True, True), "sco%d" % t)
        wait(S, "sco%d" % t)
        up(S.activation(T.sg[:, NB * t:NB * t + NB], T.psc[:, bank:bank + NB], AF.Sign, bias=-1e-30, scale=-1.0, accum_out=T.cnt[:, t:t + 1]), "act%d" % t)
        vw()
        wait(V, "act%d" % t)
        v(V.tensor_scalar(T.idx[:, 4 * t:4 * t + 4:2], T.base[:, t:2 * R:R], T.cnt[:, t:t + 1], 1.0 / 512, AL.subtract, AL.mult))
        vw()
        if not last:
            v(V.tensor_copy(T.offs[:, 16 * t:16 * t + 16], T.lw[:, PW + 16 * t:PW + 16 * t + 2 * LC].indirect(T.idx[:, 4 * t + 2:4 * t + 3])), "ofr%d" % t)
            wait(V, "ofr%d" % t)
            oc = T.offs[:, 16 * t:16 * t + LC]
            v(V.tensor_copy(T["sndc%d" % (t + 1)][:, :].bitcast(dt.uint32), wc[:, :].bitcast(dt.uint32).indirect(oc)), "pc%d" % (t + 1))
            wait(S, "ofr%d" % t)
            up(S.activation(T["snds%d" % (t + 1)][:, :], ws[:, :].indirect(oc), AF.Copy), "ps%d" % (t + 1))
            send(t + 1)
            if t + 2 < R:
                fill(t + 2)
        v(V.tensor_copy(T.offt[:, 16 * t:16 * t + 16], T.lw[:, 0:PW].indirect(T.idx[:, 4 * t:4 * t + 1])), "ew%d" % t)
        wait(V, "ew%d" % t)
        wait(S, "ew%d" % t)
        if last:
            break
        oc = T.offt[:, 16 * t:16 * t + KC]
        v(V.tensor_copy(nc[:, NB:WIN].bitcast(dt.uint32), wc[:, :].bitcast(dt.uint32).indirect(oc)), "tc%d" % t)
        up(S.activation(ns[:, NB:WIN], ws[:, :].indirect(oc), AF.Copy), "ts%d" % t)
        lists_begin(t + 1)
        quantize_w(t)
        if t == R - 2:
            quantize_w(t + 1)
        lists_end(t + 1)
        wait(X, "tc%d" % t)
        wait(X, "ts%d" % t)
        wait(X, "wq%d" % t)
        if t >= 3:
            wait(X, "ev%d" % (t - 3))
        for o in range(O):
            i = O * t + o
            product(i, i % 6, (0, K), (nc, ns), "ym%d" % t)
        wait(S, "ym%d" % t)
        for o in range(O):
            i = O * t + o
            up(S.activation(T.ysb[:, K * i:K * i + K], T.psy[:, 512 * (i % 6):512 * (i % 6) + K], AF.Copy), "ev%d" % t)
        between(t + 1)

    t = R - 1
    for h in range(2):
        oc = T.offt[:, 16 * t + KC // 2 * h:16 * t + KC // 2 * (h + 1)]
        at = slice(NB + HK * h, NB + HK * h + HK)
        v(V.tensor_copy(nc[:, at].bitcast(dt.uint32), wc[:, :].bitcast(dt.uint32).indirect(oc)), "lc%d" % h)
        up(S.activation(ns[:, at], ws[:, :].indirect(oc), AF.Copy), "ls%d" % h)
    wait(X, "wq%d" % t)
    wait(X, "ev1")
    wait(X, "ev2")
    for h in range(2):
        wait(X, "lc%d" % h)
        wait(X, "ls%d" % h)
        for o in range(O):
            product(O * t + o, 2 + 2 * h + o, (HK * h, HK * h + HK), (nc, ns), "lm%d%d" % (h, o))
    for h in range(2):
        for o in range(O):
            p = 512 * (2 + 2 * h + o)
            c = K * (O * t + o) + HK * h
            wait(V if o else S, "lm%d%d" % (h, o))
            if o:
                v(V.tensor_copy(T.ysb[:, c:c + HK], T.psy[:, p:p + HK]), "le%d%d" % (h, o))
            else:
                up(S.activation(T.ysb[:, c:c + HK], T.psy[:, p:p + HK], AF.Copy), "le%d%d" % (h, o))
    for h in range(2):
        for o in range(O):
            c = K * (O * t + o) + HK * h
            on = S if h == 1 and o == 0 else Y
            wait(on, "le%d%d" % (h, o))
            up(on.dma_start(T.y[:, c:c + HK], T.ysb[:, c:c + HK]), "kq" if on is S else "yl", 16)
    for name in total:
        if waited.get(name, 0) < total[name]:
            wait(Y, name)
